import numpy as np
import ml_dtypes


def mxq(x, axis, fmt="e4m3"):
    dtype, down = {"e4m3": (ml_dtypes.float8_e4m3fn, 7), "e5m2": (ml_dtypes.float8_e5m2, 14)}[fmt]
    v = np.moveaxis(np.asarray(x, np.float32).astype(ml_dtypes.bfloat16).astype(np.float64), axis, -1)
    blocks = v.reshape(v.shape[:-1] + (-1, 32))
    amax = np.abs(blocks).max(-1, keepdims=True)
    byte = np.maximum(np.where(amax > 0, np.frexp(amax)[1] - 1 + 127, 0) - down, 1)
    scale = np.exp2(byte - 127.0)
    codes = (blocks / scale).astype(np.float32).astype(dtype).astype(np.float64)
    return np.moveaxis((codes * scale).reshape(v.shape), -1, axis)


WIDE = False


def mx_kscale(k):
    if not WIDE:
        return np.ones(k)
    levels = np.array([10, -10, 5, -5, 0])
    if k % 512:
        return np.exp2(np.random.permutation(np.resize(levels, k // 32))).repeat(32)
    a = np.empty((k // 512, 16))
    for p in range(k // 512):
        a[p, :8] = np.random.permutation(np.resize(levels, 8))
        for g in range(8):
            far = levels[np.abs(levels - a[p, g]) >= 10]
            a[p, g + 8] = far[np.random.randint(len(far))]
    return np.exp2(a.ravel()).repeat(32)


def f64(x):
    return np.asarray(x).astype(np.float64)


def striped8(idx):
    return np.concatenate([v.reshape(-1, 16).T for v in idx]).astype(np.uint16)


def unstriped8(offs):
    return np.stack([offs[16 * g:16 * g + 16].T.reshape(-1) for g in range(8)]).astype(np.int64)


def gelu(v):
    return 0.5 * v * (1.0 + np.tanh(np.sqrt(2.0 / np.pi) * (v + 0.044715 * v**3)))


K, M, T, S = 1536, 512, 1024, 512


def setup_inputs():
    n = np.random.standard_normal
    s = mx_kscale(K)[:, None]
    return {
        "xT": (n((K, T)) * s).astype(np.float32),
        "w": (n((K, M)) / np.sqrt(K) / s).astype(np.float32),
        "wgt": np.repeat(np.random.uniform(0.5, 2.0, (8, S)), 16, axis=0).astype(np.float32),
        "b": (0.3 * n(512)).astype(np.float32),
        "wgo": np.repeat(np.random.uniform(0.5, 2.0, (8, S)), 16, axis=0).astype(np.float32),
        "offs": striped8(np.stack([np.random.permutation(T)[:S] for _ in range(8)])),
        "offs2": striped8(np.stack([np.random.permutation(T)[:S] for _ in range(8)])),
    }


def reference(xT, w, wgt, b, wgo, offs, offs2):
    idx = unstriped8(offs)
    group = np.arange(K) % 512 // 64
    xg = f64(wgt)[np.arange(K) // 4 % 128] * f64(xT)[np.arange(K)[:, None], idx[group]]
    xT_ = mxq(xg, 0, "e4m3")
    w_ = mxq(f64(w), 0, "e4m3")
    y = w_.T @ xT_
    place = unstriped8(offs2)[np.arange(M) % 128 // 16]
    out = np.zeros((M, T))
    out[np.arange(M)[:, None], place] = f64(wgo)[np.arange(M) % 128] * (gelu(y + f64(b)[:, None]))
    return out

@@ -1,0 +1,240 @@
+from contextlib import ExitStack
+
+import concourse.mybir as mybir
+from concourse.masks import make_identity
+
+K, M, T, S = 1536, 512, 1024, 512
+FLOPS = 2 * K * M * S
+
+F32 = mybir.dt.float32
+BF16 = mybir.dt.bfloat16
+U32 = mybir.dt.uint32
+U16 = mybir.dt.uint16
+U8 = mybir.dt.uint8
+FP8X4 = mybir.dt.float8_e4m3fn_x4
+MULT = mybir.AluOpType.mult
+GELU = mybir.ActivationFunctionType.Gelu_apprx_tanh
+
+P = 128
+PACK = 4
+K_PASS = P * PACK
+PASSES = K // K_PASS
+HALVES = 2
+ENTRIES = S // HALVES
+LIST_COLS = ENTRIES // 16
+M_TILES = M // P
+W_COLS = M // HALVES
+COPY_RUN = 4
+ALIGN = 64
+
+
+def tile_list_hboth_gelu_kernel(tc, xT, w, wgt, b, wgo, offs, offs2, out):
+    nc = tc.nc
+    with ExitStack() as ctx:
+        keep = ctx.enter_context(tc.tile_pool(name="keep", bufs=1))
+        psum = ctx.enter_context(tc.psum_pool(name="psum", bufs=1))
+
+        lists_in = keep.tile([P, S // 16], U16, name="lists_in")
+        lists_out = keep.tile([P, S // 16], U16, name="lists_out")
+        bias_rows = keep.tile([P, P], F32, name="bias_rows")
+        ident = keep.tile([P, P], F32, name="ident")
+        bias = keep.tile([P, M_TILES], F32, name="bias")
+        scratch = keep.tile([P, 2], F32, name="scratch")
+        wgt_half = [
+            keep.tile([P, ENTRIES], F32, name=f"wgt_half{h}", tag=f"wgt_half{h}", align_bytes=ALIGN)
+            for h in range(HALVES)
+        ]
+        wgt_late = keep.tile([P, ENTRIES], F32, name="wgt_late", tag="wgt_late", align_bytes=ALIGN)
+        wgo_half = [keep.tile([P, ENTRIES], F32, name=f"wgo_half{h}") for h in range(HALVES)]
+        x = [[keep.tile([P, T], F32, name=f"x{a}_{i}") for i in range(PACK)] for a in range(PASSES)]
+        w_raw = [
+            [keep.tile([P, PACK, W_COLS], F32, name=f"w_raw{a}_{c}") for c in range(HALVES)] for a in range(PASSES)
+        ]
+        window = [keep.tile([P, T], F32, name=f"window{m}") for m in range(M_TILES)]
+        picked = [
+            [keep.tile([P, PACK, ENTRIES], F32, name=f"picked{a}_{h}") for h in range(HALVES)] for a in range(PASSES)
+        ]
+        x_bf = [keep.tile([P, S, PACK], BF16, name=f"x_bf{a}", align_bytes=ALIGN) for a in range(PASSES)]
+        w_bf = [
+            [keep.tile([P, W_COLS, PACK], BF16, name=f"w_bf{a}_{c}", align_bytes=ALIGN) for c in range(HALVES)]
+            for a in range(PASSES)
+        ]
+        second_codes = keep.tile(
+            [P, (PASSES - 1) * ENTRIES], U32, name="second_codes", tag="wgt_late", align_bytes=ALIGN
+        )
+        x_codes = [
+            [
+                keep.tile([P, ENTRIES], U32, name="x_codes0_0", tag="wgt_half1", align_bytes=ALIGN)[:],
+                second_codes[:, 0:ENTRIES],
+            ],
+            [
+                keep.tile([P, ENTRIES], U32, name="x_codes1_0", tag="wgt_half0", align_bytes=ALIGN)[:],
+                second_codes[:, ENTRIES : 2 * ENTRIES],
+            ],
+            [keep.tile([P, ENTRIES], U32, name=f"x_codes2_{h}", align_bytes=ALIGN)[:] for h in range(HALVES)],
+        ]
+        x_scales = [keep.tile([P, S], U8, name=f"x_scales{a}", align_bytes=ALIGN) for a in range(PASSES)]
+        w_codes = [
+            [keep.tile([P, W_COLS], U32, name=f"w_codes{a}_{c}", align_bytes=ALIGN) for c in range(HALVES)]
+            for a in range(PASSES)
+        ]
+        w_scales = [
+            [keep.tile([P, W_COLS], U8, name=f"w_scales{a}_{c}", align_bytes=ALIGN) for c in range(HALVES)]
+            for a in range(PASSES)
+        ]
+        y = [keep.tile([P, S], F32, name=f"y{m}") for m in range(M_TILES)]
+        bias_bank = psum.tile([P, P], F32, name="bias_bank", tag=f"acc{M_TILES - 1}_{HALVES - 1}")
+        acc = [
+            [psum.tile([P, ENTRIES], F32, name=f"acc{m}_{h}", tag=f"acc{m}_{h}") for h in range(HALVES)]
+            for m in range(M_TILES)
+        ]
+
+        def half(h):
+            return slice(h * ENTRIES, (h + 1) * ENTRIES)
+
+        def half_list(h):
+            return slice(h * LIST_COLS, (h + 1) * LIST_COLS)
+
+        def load_x(a, i):
+            planes = xT[a * K_PASS : (a + 1) * K_PASS, :].rearrange("(p i) t -> p i t", i=PACK)
+            nc.sync.dma_start(out=x[a][i][:], in_=planes[:, i, :])
+
+        def load_w(a, c):
+            rows = w[a * K_PASS : (a + 1) * K_PASS, c * W_COLS : (c + 1) * W_COLS]
+            nc.sync.dma_start(out=w_raw[a][c][:], in_=rows.rearrange("(p i) n -> p i n", i=PACK))
+
+        def gather(a, i, h):
+            late = a == PASSES - 1 and h == 1 and i < 2
+            nc.vector.tensor_tensor(
+                picked[a][h][:, i, :],
+                x[a][i][:].indirect(lists_in[:, half_list(h)]),
+                (wgt_late if late else wgt_half[h])[:],
+                MULT,
+            )
+
+        def interleave(copy, grouped, planes):
+            copy(
+                out=grouped.rearrange("p (c r) i -> p c i r", r=COPY_RUN),
+                in_=planes.rearrange("p i (c r) -> p c i r", r=COPY_RUN),
+            )
+
+        def round_x(a, h, scalar_cols):
+            grouped = x_bf[a][:, half(h), :]
+            interleave(nc.scalar.copy, grouped[:, 0:scalar_cols, :], picked[a][h][:, :, 0:scalar_cols])
+            if scalar_cols < ENTRIES:
+                rest = slice(scalar_cols, ENTRIES)
+                interleave(nc.vector.tensor_copy, grouped[:, rest, :], picked[a][h][:, :, rest])
+
+        def quantize_x(a, h):
+            nc.vector.quantize_mx(
+                out=x_codes[a][h].bitcast(FP8X4),
+                scales=x_scales[a][:, half(h)],
+                in_=x_bf[a][:, half(h), :].rearrange("p j i -> p (j i)"),
+            )
+
+        def prepare_w(a, c, scalar_cols):
+            if scalar_cols > 0:
+                interleave(nc.scalar.copy, w_bf[a][c][:, 0:scalar_cols, :], w_raw[a][c][:, :, 0:scalar_cols])
+            if scalar_cols < W_COLS:
+                rest = slice(scalar_cols, W_COLS)
+                interleave(nc.vector.tensor_copy, w_bf[a][c][:, rest, :], w_raw[a][c][:, :, rest])
+            nc.vector.quantize_mx(
+                out=w_codes[a][c][:].bitcast(FP8X4),
+                scales=w_scales[a][c][:],
+                in_=w_bf[a][c][:].rearrange("p n i -> p (n i)"),
+            )
+
+        def project(m, h):
+            c, n0 = m * P // W_COLS, m * P % W_COLS
+            for a in range(PASSES):
+                nc.tensor.matmul_mx(
+                    out=acc[m][h][:],
+                    lhsT=w_codes[a][c][:, n0 : n0 + P].bitcast(FP8X4),
+                    lhsT_scale=w_scales[a][c][:, n0 : n0 + P],
+                    rhs=x_codes[a][h].bitcast(FP8X4),
+                    rhs_scale=x_scales[a][:, half(h)],
+                    start=(a == 0),
+                    stop=(a == PASSES - 1),
+                )
+            nc.scalar.activation(y[m][:, half(h)], acc[m][h][:], GELU, bias=bias[:, m : m + 1])
+
+        def scatter(m, h):
+            nc.vector.tensor_tensor(
+                window[m][:].indirect(lists_out[:, half_list(h)]),
+                y[m][:, half(h)],
+                wgo_half[h][:],
+                MULT,
+            )
+
+        def store(m):
+            nc.sync.dma_start(out=out[m * P : (m + 1) * P, :], in_=window[m][:])
+
+        nc.gpsimd.memset(scratch[:], 0.0)
+        nc.gpsimd.memset(bias_rows[:], 0.0)
+        nc.scalar.activation(scratch[:, 1:2], scratch[:, 0:1], GELU)
+
+        nc.sync.dma_start(lists_in[:], offs)
+        nc.scalar.dma_start(out=wgt_half[0][:], in_=wgt[:, half(0)])
+        load_x(0, 0)
+        nc.sync.dma_start(out=wgt_half[1][:], in_=wgt[:, half(1)])
+        nc.sync.dma_start(lists_out[:], offs2)
+        nc.sync.dma_start(out=bias_rows[0:M_TILES, :], in_=b.rearrange("(m p) -> m p", p=P))
+        for a in range(PASSES):
+            for i in range(PACK):
+                if (a, i) != (0, 0):
+                    load_x(a, i)
+        for a in range(PASSES):
+            load_w(a, 0)
+        load_w(0, 1)
+        nc.sync.dma_start(out=wgo_half[0][:], in_=wgo[:, half(0)])
+        nc.sync.dma_start(out=wgt_late[:], in_=wgt[:, half(1)])
+        for a in range(1, PASSES):
+            load_w(a, 1)
+        nc.sync.dma_start(out=wgo_half[1][:], in_=wgo[:, half(1)])
+
+        nc.vector.memset(window[0][:], 0.0)
+        nc.vector.memset(window[1][:], 0.0)
+        make_identity(nc, ident[:])
+        nc.gpsimd.memset(window[2][:], 0.0)
+        nc.gpsimd.memset(window[3][:], 0.0)
+
+        nc.tensor.transpose(bias_bank[:], bias_rows[:], ident[:])
+        nc.scalar.copy(out=bias[:], in_=bias_bank[:, 0:M_TILES])
+
+        for a in range(PASSES):
+            for i in range(PACK):
+                for h in range(HALVES):
+                    gather(a, i, h)
+            if a < PASSES - 1:
+                for h in range(HALVES):
+                    round_x(a, h, ENTRIES)
+                for h in range(HALVES):
+                    quantize_x(a, h)
+            else:
+                for h in range(HALVES):
+                    round_x(a, h, ENTRIES // 2)
+                    quantize_x(a, h)
+
+        prepare_w(0, 0, 0)
+        prepare_w(1, 0, W_COLS)
+        prepare_w(2, 0, W_COLS // 2)
+
+        project(0, 0)
+        project(1, 0)
+        prepare_w(0, 1, W_COLS)
+        scatter(0, 0)
+        scatter(1, 0)
+        project(0, 1)
+        prepare_w(1, 1, W_COLS)
+        prepare_w(2, 1, W_COLS)
+        project(1, 1)
+        for m in (0, 1):
+            scatter(m, 1)
+            store(m)
+        for h in range(HALVES):
+            for m in (2, 3):
+                project(m, h)
+            for m in (2, 3):
+                scatter(m, h)
+                if h == HALVES - 1:
+                    store(m)

@@ -19,13 +19,11 @@ P = 128
 PACK = 4
 K_PASS = P * PACK
 PASSES = K // K_PASS
-HALVES = 2
-ENTRIES = S // HALVES
-LIST_COLS = ENTRIES // 16
+LAST = PASSES - 1
 M_TILES = M // P
-W_COLS = M // HALVES
 COPY_RUN = 4
 ALIGN = 64
+PIECES = (slice(0, 128), slice(128, 256), slice(256, 512))
 
 
 def tile_list_hboth_gelu_kernel(tc, xT, w, wgt, b, wgo, offs, offs2, out):
@@ -34,83 +32,65 @@ def tile_list_hboth_gelu_kernel(tc, xT, w, wgt, b, wgo, offs, offs2, out):
         keep = ctx.enter_context(tc.tile_pool(name="keep", bufs=1))
         psum = ctx.enter_context(tc.psum_pool(name="psum", bufs=1))
 
+        def sbuf(shape, dtype, name, tag=None):
+            return keep.tile(shape, dtype, name=name, tag=tag or name, align_bytes=ALIGN)
+
         lists_in = keep.tile([P, S // 16], U16, name="lists_in")
         lists_out = keep.tile([P, S // 16], U16, name="lists_out")
-        bias_rows = keep.tile([P, P], F32, name="bias_rows")
-        ident = keep.tile([P, P], F32, name="ident")
-        bias = keep.tile([P, M_TILES], F32, name="bias")
-        scratch = keep.tile([P, 2], F32, name="scratch")
-        wgt_half = [
-            keep.tile([P, ENTRIES], F32, name=f"wgt_half{h}", tag=f"wgt_half{h}", align_bytes=ALIGN)
-            for h in range(HALVES)
-        ]
-        wgt_late = keep.tile([P, ENTRIES], F32, name="wgt_late", tag="wgt_late", align_bytes=ALIGN)
-        wgo_half = [keep.tile([P, ENTRIES], F32, name=f"wgo_half{h}") for h in range(HALVES)]
-        x = [[keep.tile([P, T], F32, name=f"x{a}_{i}") for i in range(PACK)] for a in range(PASSES)]
-        w_raw = [
-            [keep.tile([P, PACK, W_COLS], F32, name=f"w_raw{a}_{c}") for c in range(HALVES)] for a in range(PASSES)
-        ]
+        bias_rows = sbuf([P, P], F32, "bias_rows")
+        ident = sbuf([P, P], F32, "ident")
+        bias = sbuf([P, M_TILES], F32, "bias")
+        scratch = sbuf([P, 2], F32, "scratch")
+        wgt_sb = sbuf([P, S], F32, "wgt_sb")
+        wgo_sb = sbuf([P, S], F32, "wgo_sb")
+        x = [[sbuf([P, T], F32, f"x{a}_{i}") for i in range(PACK)] for a in range(PASSES)]
+        w_raw = [[sbuf([P, PACK, P], F32, f"w_raw{m}_{a}") for a in range(PASSES)] for m in range(M_TILES)]
         window = [keep.tile([P, T], F32, name=f"window{m}") for m in range(M_TILES)]
-        picked = [
-            [keep.tile([P, PACK, ENTRIES], F32, name=f"picked{a}_{h}") for h in range(HALVES)] for a in range(PASSES)
+        picked = [sbuf([P, PACK, S], F32, f"picked{a}") for a in range(LAST)]
+        picked_first = sbuf([P, PACK, 128], F32, "picked_first")
+        picked_rest = sbuf([P, PACK, S - 128], F32, "picked_rest")
+        x_bf = sbuf([P, LAST, S, PACK], BF16, "x_bf")
+        x_bf_last = [
+            sbuf([P, 128, PACK], BF16, "x_bf_last0"),
+            sbuf([P, 128, PACK], BF16, "x_bf_last1"),
+            sbuf([P, 256, PACK], BF16, "x_bf_last2", tag="picked_first"),
         ]
-        x_bf = [keep.tile([P, S, PACK], BF16, name=f"x_bf{a}", align_bytes=ALIGN) for a in range(PASSES)]
-        w_bf = [
-            [keep.tile([P, W_COLS, PACK], BF16, name=f"w_bf{a}_{c}", align_bytes=ALIGN) for c in range(HALVES)]
-            for a in range(PASSES)
+        w_bf = [[sbuf([P, P, PACK], BF16, f"w_bf{m}_{a}") for a in range(PASSES)] for m in range(M_TILES)]
+        x_codes_early = sbuf([P, LAST * S], U32, "x_codes_early", tag=f"x{LAST}_{PACK - 2}")
+        x_scales_early = sbuf([P, LAST * S], U8, "x_scales_early")
+        x_codes_last = sbuf([P, S], U32, "x_codes_last")
+        x_scales_last = sbuf([P, S], U8, "x_scales_last")
+        x_codes = [x_codes_early[:, a * S : (a + 1) * S] for a in range(LAST)] + [x_codes_last[:]]
+        x_scales = [x_scales_early[:, a * S : (a + 1) * S] for a in range(LAST)] + [x_scales_last[:]]
+        w_codes = [[sbuf([P, P], U32, f"w_codes{m}_{a}") for a in range(PASSES)] for m in range(M_TILES)]
+        w_scales = [[sbuf([P, P], U8, f"w_scales{m}_{a}") for a in range(PASSES)] for m in range(M_TILES)]
+        y_first = [
+            sbuf([P, 128], F32, "y_first0"),
+            sbuf([P, 128], F32, "y_first1"),
+            sbuf([P, 256], F32, "y_first2", tag=f"w_raw1_{LAST}"),
         ]
-        second_codes = keep.tile(
-            [P, (PASSES - 1) * ENTRIES], U32, name="second_codes", tag="wgt_late", align_bytes=ALIGN
-        )
-        x_codes = [
-            [
-                keep.tile([P, ENTRIES], U32, name="x_codes0_0", tag="wgt_half1", align_bytes=ALIGN)[:],
-                second_codes[:, 0:ENTRIES],
-            ],
-            [
-                keep.tile([P, ENTRIES], U32, name="x_codes1_0", tag="wgt_half0", align_bytes=ALIGN)[:],
-                second_codes[:, ENTRIES : 2 * ENTRIES],
-            ],
-            [keep.tile([P, ENTRIES], U32, name=f"x_codes2_{h}", align_bytes=ALIGN)[:] for h in range(HALVES)],
+        y = [None] + [
+            sbuf([P, S], F32, f"y{m}", tag=f"w_raw{m + 1}_{LAST}" if m + 1 < M_TILES else None)
+            for m in range(1, M_TILES)
         ]
-        x_scales = [keep.tile([P, S], U8, name=f"x_scales{a}", align_bytes=ALIGN) for a in range(PASSES)]
-        w_codes = [
-            [keep.tile([P, W_COLS], U32, name=f"w_codes{a}_{c}", align_bytes=ALIGN) for c in range(HALVES)]
-            for a in range(PASSES)
-        ]
-        w_scales = [
-            [keep.tile([P, W_COLS], U8, name=f"w_scales{a}_{c}", align_bytes=ALIGN) for c in range(HALVES)]
-            for a in range(PASSES)
-        ]
-        y = [keep.tile([P, S], F32, name=f"y{m}") for m in range(M_TILES)]
-        bias_bank = psum.tile([P, P], F32, name="bias_bank", tag=f"acc{M_TILES - 1}_{HALVES - 1}")
-        acc = [
-            [psum.tile([P, ENTRIES], F32, name=f"acc{m}_{h}", tag=f"acc{m}_{h}") for h in range(HALVES)]
-            for m in range(M_TILES)
-        ]
+        bias_bank = psum.tile([P, P], F32, name="bias_bank")
+        acc_first = [psum.tile([P, c.stop - c.start], F32, name=f"acc_first{n}") for n, c in enumerate(PIECES)]
+        acc = [None] + [psum.tile([P, S], F32, name=f"acc{m}") for m in range(1, M_TILES)]
 
-        def half(h):
-            return slice(h * ENTRIES, (h + 1) * ENTRIES)
-
-        def half_list(h):
-            return slice(h * LIST_COLS, (h + 1) * LIST_COLS)
+        def list_cols(entries):
+            return slice(entries.start // 16, entries.stop // 16)
 
         def load_x(a, i):
             planes = xT[a * K_PASS : (a + 1) * K_PASS, :].rearrange("(p i) t -> p i t", i=PACK)
             nc.sync.dma_start(out=x[a][i][:], in_=planes[:, i, :])
 
-        def load_w(a, c):
-            rows = w[a * K_PASS : (a + 1) * K_PASS, c * W_COLS : (c + 1) * W_COLS]
-            nc.sync.dma_start(out=w_raw[a][c][:], in_=rows.rearrange("(p i) n -> p i n", i=PACK))
+        def load_w(m):
+            for a in range(PASSES):
+                rows = w[a * K_PASS : (a + 1) * K_PASS, m * P : (m + 1) * P]
+                nc.sync.dma_start(out=w_raw[m][a][:], in_=rows.rearrange("(p i) n -> p i n", i=PACK))
 
-        def gather(a, i, h):
-            late = a == PASSES - 1 and h == 1 and i < 2
-            nc.vector.tensor_tensor(
-                picked[a][h][:, i, :],
-                x[a][i][:].indirect(lists_in[:, half_list(h)]),
-                (wgt_late if late else wgt_half[h])[:],
-                MULT,
-            )
+        def gather(dst, plane, entries):
+            nc.vector.tensor_tensor(dst, plane[:].indirect(lists_in[:, list_cols(entries)]), wgt_sb[:, entries], MULT)
 
         def interleave(copy, grouped, planes):
             copy(
@@ -118,123 +98,99 @@ def tile_list_hboth_gelu_kernel(tc, xT, w, wgt, b, wgo, offs, offs2, out):
                 in_=planes.rearrange("p i (c r) -> p c i r", r=COPY_RUN),
             )
 
-        def round_x(a, h, scalar_cols):
-            grouped = x_bf[a][:, half(h), :]
-            interleave(nc.scalar.copy, grouped[:, 0:scalar_cols, :], picked[a][h][:, :, 0:scalar_cols])
-            if scalar_cols < ENTRIES:
-                rest = slice(scalar_cols, ENTRIES)
-                interleave(nc.vector.tensor_copy, grouped[:, rest, :], picked[a][h][:, :, rest])
+        def quantize(codes, scales, grouped):
+            nc.vector.quantize_mx(out=codes.bitcast(FP8X4), scales=scales, in_=grouped)
 
-        def quantize_x(a, h):
-            nc.vector.quantize_mx(
-                out=x_codes[a][h].bitcast(FP8X4),
-                scales=x_scales[a][:, half(h)],
-                in_=x_bf[a][:, half(h), :].rearrange("p j i -> p (j i)"),
-            )
+        def prepare_w(m):
+            for a in range(PASSES):
+                interleave(nc.scalar.copy, w_bf[m][a][:], w_raw[m][a][:])
+                quantize(w_codes[m][a][:], w_scales[m][a][:], w_bf[m][a][:].rearrange("p n i -> p (n i)"))
 
-        def prepare_w(a, c, scalar_cols):
-            if scalar_cols > 0:
-                interleave(nc.scalar.copy, w_bf[a][c][:, 0:scalar_cols, :], w_raw[a][c][:, :, 0:scalar_cols])
-            if scalar_cols < W_COLS:
-                rest = slice(scalar_cols, W_COLS)
-                interleave(nc.vector.tensor_copy, w_bf[a][c][:, rest, :], w_raw[a][c][:, :, rest])
-            nc.vector.quantize_mx(
-                out=w_codes[a][c][:].bitcast(FP8X4),
-                scales=w_scales[a][c][:],
-                in_=w_bf[a][c][:].rearrange("p n i -> p (n i)"),
-            )
-
-        def project(m, h):
-            c, n0 = m * P // W_COLS, m * P % W_COLS
+        def project(m, entries, bank, dst):
             for a in range(PASSES):
                 nc.tensor.matmul_mx(
-                    out=acc[m][h][:],
-                    lhsT=w_codes[a][c][:, n0 : n0 + P].bitcast(FP8X4),
-                    lhsT_scale=w_scales[a][c][:, n0 : n0 + P],
-                    rhs=x_codes[a][h].bitcast(FP8X4),
-                    rhs_scale=x_scales[a][:, half(h)],
+                    out=bank[:],
+                    lhsT=w_codes[m][a][:].bitcast(FP8X4),
+                    lhsT_scale=w_scales[m][a][:],
+                    rhs=x_codes[a][:, entries].bitcast(FP8X4),
+                    rhs_scale=x_scales[a][:, entries],
                     start=(a == 0),
-                    stop=(a == PASSES - 1),
+                    stop=(a == LAST),
                 )
-            nc.scalar.activation(y[m][:, half(h)], acc[m][h][:], GELU, bias=bias[:, m : m + 1])
+            nc.scalar.activation(dst[:], bank[:], GELU, bias=bias[:, m : m + 1])
 
-        def scatter(m, h):
+        def scatter(m, entries, src):
             nc.vector.tensor_tensor(
-                window[m][:].indirect(lists_out[:, half_list(h)]),
-                y[m][:, half(h)],
-                wgo_half[h][:],
-                MULT,
+                window[m][:].indirect(lists_out[:, list_cols(entries)]), src[:], wgo_sb[:, entries], MULT
             )
 
         def store(m):
             nc.sync.dma_start(out=out[m * P : (m + 1) * P, :], in_=window[m][:])
+
+        everything = slice(0, S)
 
         nc.gpsimd.memset(scratch[:], 0.0)
         nc.gpsimd.memset(bias_rows[:], 0.0)
         nc.scalar.activation(scratch[:, 1:2], scratch[:, 0:1], GELU)
 
         nc.sync.dma_start(lists_in[:], offs)
-        nc.scalar.dma_start(out=wgt_half[0][:], in_=wgt[:, half(0)])
-        load_x(0, 0)
-        nc.sync.dma_start(out=wgt_half[1][:], in_=wgt[:, half(1)])
-        nc.sync.dma_start(lists_out[:], offs2)
-        nc.sync.dma_start(out=bias_rows[0:M_TILES, :], in_=b.rearrange("(m p) -> m p", p=P))
+        nc.scalar.dma_start(out=wgt_sb[:, 0 : S // 2], in_=wgt[:, 0 : S // 2])
         for a in range(PASSES):
             for i in range(PACK):
-                if (a, i) != (0, 0):
-                    load_x(a, i)
-        for a in range(PASSES):
-            load_w(a, 0)
-        load_w(0, 1)
-        nc.sync.dma_start(out=wgo_half[0][:], in_=wgo[:, half(0)])
-        nc.sync.dma_start(out=wgt_late[:], in_=wgt[:, half(1)])
-        for a in range(1, PASSES):
-            load_w(a, 1)
-        nc.sync.dma_start(out=wgo_half[1][:], in_=wgo[:, half(1)])
+                if (a, i) == (LAST, PACK - 1):
+                    load_w(0)
+                load_x(a, i)
+                if (a, i) == (0, 0):
+                    nc.sync.dma_start(out=wgt_sb[:, S // 2 : S], in_=wgt[:, S // 2 : S])
+                if (a, i) == (0, 1):
+                    nc.sync.dma_start(lists_out[:], offs2)
+                    nc.sync.dma_start(out=bias_rows[0:M_TILES, :], in_=b.rearrange("(m p) -> m p", p=P))
+        nc.sync.dma_start(out=wgo_sb[:], in_=wgo)
+        for m in range(1, M_TILES):
+            load_w(m)
 
-        nc.vector.memset(window[0][:], 0.0)
-        nc.vector.memset(window[1][:], 0.0)
+        for m in range(M_TILES - 1):
+            nc.vector.memset(window[m][:].bitcast(U32), 0)
         make_identity(nc, ident[:])
-        nc.gpsimd.memset(window[2][:], 0.0)
-        nc.gpsimd.memset(window[3][:], 0.0)
+        nc.gpsimd.memset(window[M_TILES - 1][:], 0.0)
 
         nc.tensor.transpose(bias_bank[:], bias_rows[:], ident[:])
         nc.scalar.copy(out=bias[:], in_=bias_bank[:, 0:M_TILES])
 
-        for a in range(PASSES):
+        for a in range(LAST):
             for i in range(PACK):
-                for h in range(HALVES):
-                    gather(a, i, h)
-            if a < PASSES - 1:
-                for h in range(HALVES):
-                    round_x(a, h, ENTRIES)
-                for h in range(HALVES):
-                    quantize_x(a, h)
-            else:
-                for h in range(HALVES):
-                    round_x(a, h, ENTRIES // 2)
-                    quantize_x(a, h)
+                for entries in (slice(0, S // 2), slice(S // 2, S)) if (a, i) == (0, 0) else (everything,):
+                    gather(picked[a][:, i, entries], x[a][i], entries)
+            interleave(nc.scalar.copy, x_bf[:, a, :, :], picked[a][:])
+        for i in range(PACK):
+            gather(picked_first[:, i, :], x[LAST][i], PIECES[0])
+            gather(picked_rest[:, i, :], x[LAST][i], slice(128, S))
+            if i == PACK - 2:
+                quantize(x_codes_early[:], x_scales_early[:], x_bf[:].rearrange("p a j i -> p (a j i)"))
+                prepare_w(0)
 
-        prepare_w(0, 0, 0)
-        prepare_w(1, 0, W_COLS)
-        prepare_w(2, 0, W_COLS // 2)
+        def quantize_last(n):
+            quantize(
+                x_codes_last[:, PIECES[n]], x_scales_last[:, PIECES[n]], x_bf_last[n][:].rearrange("p j i -> p (j i)")
+            )
 
-        project(0, 0)
-        project(1, 0)
-        prepare_w(0, 1, W_COLS)
-        scatter(0, 0)
-        scatter(1, 0)
-        project(0, 1)
-        prepare_w(1, 1, W_COLS)
-        prepare_w(2, 1, W_COLS)
-        project(1, 1)
-        for m in (0, 1):
-            scatter(m, 1)
+        interleave(nc.scalar.copy, x_bf_last[0][:], picked_first[:])
+        quantize_last(0)
+        interleave(nc.scalar.copy, x_bf_last[1][:], picked_rest[:, :, 0:128])
+        interleave(nc.vector.tensor_copy, x_bf_last[2][:], picked_rest[:, :, 128:384])
+        quantize_last(1)
+        project(0, PIECES[0], acc_first[0], y_first[0])
+        scatter(0, PIECES[0], y_first[0])
+        quantize_last(2)
+        project(0, PIECES[1], acc_first[1], y_first[1])
+        scatter(0, PIECES[1], y_first[1])
+        prepare_w(1)
+        project(0, PIECES[2], acc_first[2], y_first[2])
+        scatter(0, PIECES[2], y_first[2])
+        store(0)
+        for m in range(1, M_TILES):
+            if m + 1 < M_TILES:
+                prepare_w(m + 1)
+            project(m, everything, acc[m], y[m])
+            scatter(m, everything, y[m])
             store(m)
-        for h in range(HALVES):
-            for m in (2, 3):
-                project(m, h)
-            for m in (2, 3):
-                scatter(m, h)
-                if h == HALVES - 1:
-                    store(m)

@@ -24,6 +24,7 @@ M_TILES = M // P
 COPY_RUN = 4
 ALIGN = 64
 PIECES = (slice(0, 128), slice(128, 256), slice(256, 512))
+WIDTHS = tuple(c.stop - c.start for c in PIECES)
 
 
 def tile_list_hboth_gelu_kernel(tc, xT, w, wgt, b, wgo, offs, offs2, out):
@@ -44,38 +45,70 @@ def tile_list_hboth_gelu_kernel(tc, xT, w, wgt, b, wgo, offs, offs2, out):
         wgt_sb = sbuf([P, S], F32, "wgt_sb")
         wgo_sb = sbuf([P, S], F32, "wgo_sb")
         x = [[sbuf([P, T], F32, f"x{a}_{i}") for i in range(PACK)] for a in range(PASSES)]
-        w_raw = [[sbuf([P, PACK, P], F32, f"w_raw{m}_{a}") for a in range(PASSES)] for m in range(M_TILES)]
+        w_raw_joint = [sbuf([P, PASSES, PACK, P], F32, f"w_raw{m}") if m >= 2 else None for m in range(M_TILES)]
+        w_raw = [
+            [
+                w_raw_joint[m][:, a, :, :] if m >= 2 else sbuf([P, PACK, P], F32, f"w_raw{m}_{a}")[:]
+                for a in range(PASSES)
+            ]
+            for m in range(M_TILES)
+        ]
         window = [keep.tile([P, T], F32, name=f"window{m}") for m in range(M_TILES)]
-        picked = [sbuf([P, PACK, S], F32, f"picked{a}") for a in range(LAST)]
-        picked_first = sbuf([P, PACK, 128], F32, "picked_first")
-        picked_rest = sbuf([P, PACK, S - 128], F32, "picked_rest")
-        x_bf = sbuf([P, LAST, S, PACK], BF16, "x_bf")
-        x_bf_last = [
-            sbuf([P, 128, PACK], BF16, "x_bf_last0"),
-            sbuf([P, 128, PACK], BF16, "x_bf_last1"),
-            sbuf([P, 256, PACK], BF16, "x_bf_last2", tag="picked_first"),
+        picked = [sbuf([P, PACK, S], F32, f"picked{a}") for a in range(PASSES)]
+        x_bf_early = [sbuf([P, LAST, WIDTHS[n], PACK], BF16, f"x_bf_early{n}") for n in range(3)]
+        x_bf_last = [sbuf([P, WIDTHS[n], PACK], BF16, f"x_bf_last{n}") for n in range(3)]
+        w_bf = [[sbuf([P, P, PACK], BF16, f"w_bf{m}_{a}") for a in range(PASSES)] for m in range(2)]
+        w_bf_joint = [sbuf([P, PASSES, P, PACK], BF16, f"w_bf{m}") if m >= 2 else None for m in range(M_TILES)]
+        codes_head = sbuf([P, LAST * P], U32, "codes_head", tag=f"x{LAST}_2")
+        codes_urgent = sbuf([P, 3 * P], U32, "codes_urgent", tag=f"w_raw0_{LAST}")
+        codes_rest = sbuf([P, PASSES * (S - P)], U32, "codes_rest", tag=f"w_bf0_{LAST}")
+        early_codes = [codes_head[:], codes_rest[:, 0:256], codes_rest[:, 256:768]]
+        last_codes = [codes_urgent[:, 2 * P : 3 * P], codes_rest[:, 768:896], codes_rest[:, 896:1152]]
+        early_scales = [sbuf([P, LAST * WIDTHS[n]], U8, f"early_scales{n}") for n in range(3)]
+        last_scales = [sbuf([P, WIDTHS[n]], U8, f"last_scales{n}") for n in range(3)]
+        x_codes = [
+            [early_codes[n][:, a * WIDTHS[n] : (a + 1) * WIDTHS[n]] for n in range(3)] for a in range(LAST)
+        ] + [last_codes]
+        x_scales = [
+            [early_scales[n][:, a * WIDTHS[n] : (a + 1) * WIDTHS[n]] for n in range(3)] for a in range(LAST)
+        ] + [[last_scales[n][:] for n in range(3)]]
+        w_codes = [
+            [
+                codes_urgent[:, (a - 1) * P : a * P]
+                if m == 0 and a > 0
+                else sbuf([P, P], U32, f"w_codes{m}_{a}", tag="x2_3" if m == 0 else None)[:]
+                for a in range(PASSES)
+            ]
+            for m in range(2)
         ]
-        w_bf = [[sbuf([P, P, PACK], BF16, f"w_bf{m}_{a}") for a in range(PASSES)] for m in range(M_TILES)]
-        x_codes_early = sbuf([P, LAST * S], U32, "x_codes_early", tag=f"x{LAST}_{PACK - 2}")
-        x_scales_early = sbuf([P, LAST * S], U8, "x_scales_early")
-        x_codes_last = sbuf([P, S], U32, "x_codes_last")
-        x_scales_last = sbuf([P, S], U8, "x_scales_last")
-        x_codes = [x_codes_early[:, a * S : (a + 1) * S] for a in range(LAST)] + [x_codes_last[:]]
-        x_scales = [x_scales_early[:, a * S : (a + 1) * S] for a in range(LAST)] + [x_scales_last[:]]
-        w_codes = [[sbuf([P, P], U32, f"w_codes{m}_{a}") for a in range(PASSES)] for m in range(M_TILES)]
-        w_scales = [[sbuf([P, P], U8, f"w_scales{m}_{a}") for a in range(PASSES)] for m in range(M_TILES)]
-        y_first = [
-            sbuf([P, 128], F32, "y_first0"),
-            sbuf([P, 128], F32, "y_first1"),
-            sbuf([P, 256], F32, "y_first2", tag=f"w_raw1_{LAST}"),
+        w_scales = [[sbuf([P, P], U8, f"w_scales{m}_{a}")[:] for a in range(PASSES)] for m in range(2)]
+        codes_joint = [sbuf([P, PASSES * P], U32, f"w_codes{m}") if m >= 2 else None for m in range(M_TILES)]
+        scales_joint = [sbuf([P, PASSES * P], U8, f"w_scales{m}") if m >= 2 else None for m in range(M_TILES)]
+        for m in range(2, M_TILES):
+            w_codes.append([codes_joint[m][:, a * P : (a + 1) * P] for a in range(PASSES)])
+            w_scales.append([scales_joint[m][:, a * P : (a + 1) * P] for a in range(PASSES)])
+        groups = (((0,), (1,), (2,)), ((0, 1), (2,)), ((0, 1, 2),), ((0, 1, 2),))
+        slots = ((None, "w_raw1_1", "w_raw1_2"), ("w_raw2", "w_raw3"), (None,), (None,))
+        y = [
+            [
+                None if (m, u) in ((1, 1), (2, 0)) else sbuf([P, sum(WIDTHS[n] for n in g)], F32, f"y{m}_{u}", tag=slots[m][u])[:]
+                for u, g in enumerate(groups[m])
+            ]
+            for m in range(M_TILES)
         ]
-        y = [None] + [
-            sbuf([P, S], F32, f"y{m}", tag=f"w_raw{m + 1}_{LAST}" if m + 1 < M_TILES else None)
-            for m in range(1, M_TILES)
+        y_late = sbuf([P, S // 2 + S], F32, "y_late", tag="w_raw3")
+        y[1].pop()
+        y[1].append(y_late[:, 0 : S // 2])
+        y[2].pop()
+        y[2].append(y_late[:, S // 2 : S // 2 + S])
+        bias_bank = psum.tile([P, P], F32, name="bias_bank", tag="acc3_0")
+        acc = [
+            [
+                psum.tile([P, sum(WIDTHS[n] for n in g)], F32, name=f"acc{m}_{u}", tag=f"acc{m}_{u}")
+                for u, g in enumerate(groups[m])
+            ]
+            for m in range(M_TILES)
         ]
-        bias_bank = psum.tile([P, P], F32, name="bias_bank")
-        acc_first = [psum.tile([P, c.stop - c.start], F32, name=f"acc_first{n}") for n, c in enumerate(PIECES)]
-        acc = [None] + [psum.tile([P, S], F32, name=f"acc{m}") for m in range(1, M_TILES)]
 
         def list_cols(entries):
             return slice(entries.start // 16, entries.stop // 16)
@@ -84,13 +117,14 @@ def tile_list_hboth_gelu_kernel(tc, xT, w, wgt, b, wgo, offs, offs2, out):
             planes = xT[a * K_PASS : (a + 1) * K_PASS, :].rearrange("(p i) t -> p i t", i=PACK)
             nc.sync.dma_start(out=x[a][i][:], in_=planes[:, i, :])
 
-        def load_w(m):
-            for a in range(PASSES):
-                rows = w[a * K_PASS : (a + 1) * K_PASS, m * P : (m + 1) * P]
-                nc.sync.dma_start(out=w_raw[m][a][:], in_=rows.rearrange("(p i) n -> p i n", i=PACK))
+        def load_w(m, a):
+            rows = w[a * K_PASS : (a + 1) * K_PASS, m * P : (m + 1) * P]
+            nc.sync.dma_start(out=w_raw[m][a], in_=rows.rearrange("(p i) n -> p i n", i=PACK))
 
-        def gather(dst, plane, entries):
-            nc.vector.tensor_tensor(dst, plane[:].indirect(lists_in[:, list_cols(entries)]), wgt_sb[:, entries], MULT)
+        def gather(a, i, entries):
+            nc.vector.tensor_tensor(
+                picked[a][:, i, entries], x[a][i][:].indirect(lists_in[:, list_cols(entries)]), wgt_sb[:, entries], MULT
+            )
 
         def interleave(copy, grouped, planes):
             copy(
@@ -101,31 +135,50 @@ def tile_list_hboth_gelu_kernel(tc, xT, w, wgt, b, wgo, offs, offs2, out):
         def quantize(codes, scales, grouped):
             nc.vector.quantize_mx(out=codes.bitcast(FP8X4), scales=scales, in_=grouped)
 
-        def prepare_w(m):
-            for a in range(PASSES):
-                interleave(nc.scalar.copy, w_bf[m][a][:], w_raw[m][a][:])
-                quantize(w_codes[m][a][:], w_scales[m][a][:], w_bf[m][a][:].rearrange("p n i -> p (n i)"))
+        def round_w(m, a, copy=nc.scalar.copy):
+            interleave(copy, w_bf[m][a][:], w_raw[m][a])
 
-        def project(m, entries, bank, dst):
-            for a in range(PASSES):
-                nc.tensor.matmul_mx(
-                    out=bank[:],
-                    lhsT=w_codes[m][a][:].bitcast(FP8X4),
-                    lhsT_scale=w_scales[m][a][:],
-                    rhs=x_codes[a][:, entries].bitcast(FP8X4),
-                    rhs_scale=x_scales[a][:, entries],
-                    start=(a == 0),
-                    stop=(a == LAST),
-                )
-            nc.scalar.activation(dst[:], bank[:], GELU, bias=bias[:, m : m + 1])
+        def quantize_w(m, a):
+            quantize(w_codes[m][a], w_scales[m][a], w_bf[m][a][:].rearrange("p n i -> p (n i)"))
 
-        def scatter(m, entries, src):
-            nc.vector.tensor_tensor(
-                window[m][:].indirect(lists_out[:, list_cols(entries)]), src[:], wgo_sb[:, entries], MULT
+        def prepare_joint(m):
+            nc.scalar.copy(
+                out=w_bf_joint[m][:].rearrange("p a (c r) i -> p a c i r", r=COPY_RUN),
+                in_=w_raw_joint[m][:].rearrange("p a i (c r) -> p a c i r", r=COPY_RUN),
             )
+            for lo, hi in ((0, LAST), (LAST, PASSES)):
+                quantize(
+                    codes_joint[m][:, lo * P : hi * P],
+                    scales_joint[m][:, lo * P : hi * P],
+                    w_bf_joint[m][:, lo:hi, :, :].rearrange("p a n i -> p (a n i)"),
+                )
 
-        def store(m):
-            nc.sync.dma_start(out=out[m * P : (m + 1) * P, :], in_=window[m][:])
+        def quantize_early(n):
+            quantize(early_codes[n], early_scales[n][:], x_bf_early[n][:].rearrange("p a j i -> p (a j i)"))
+
+        def quantize_last(n):
+            quantize(last_codes[n], last_scales[n][:], x_bf_last[n][:].rearrange("p j i -> p (j i)"))
+
+        def finish(m, u):
+            first = PIECES[groups[m][u][0]].start
+            for a in range(PASSES):
+                for n in groups[m][u]:
+                    nc.tensor.matmul_mx(
+                        out=acc[m][u][:, PIECES[n].start - first : PIECES[n].stop - first],
+                        lhsT=w_codes[m][a].bitcast(FP8X4),
+                        lhsT_scale=w_scales[m][a],
+                        rhs=x_codes[a][n].bitcast(FP8X4),
+                        rhs_scale=x_scales[a][n],
+                        start=(a == 0 and n == groups[m][u][0]),
+                        stop=(a == LAST and n == groups[m][u][-1]),
+                    )
+            nc.scalar.activation(y[m][u], acc[m][u][:], GELU, bias=bias[:, m : m + 1])
+            entries = slice(first, PIECES[groups[m][u][-1]].stop)
+            nc.vector.tensor_tensor(
+                window[m][:].indirect(lists_out[:, list_cols(entries)]), y[m][u], wgo_sb[:, entries], MULT
+            )
+            if u == len(groups[m]) - 1:
+                nc.sync.dma_start(out=out[m * P : (m + 1) * P, :], in_=window[m][:])
 
         everything = slice(0, S)
 
@@ -138,16 +191,18 @@ def tile_list_hboth_gelu_kernel(tc, xT, w, wgt, b, wgo, offs, offs2, out):
         for a in range(PASSES):
             for i in range(PACK):
                 if (a, i) == (LAST, PACK - 1):
-                    load_w(0)
+                    load_w(0, 0)
                 load_x(a, i)
                 if (a, i) == (0, 0):
                     nc.sync.dma_start(out=wgt_sb[:, S // 2 : S], in_=wgt[:, S // 2 : S])
-                if (a, i) == (0, 1):
-                    nc.sync.dma_start(lists_out[:], offs2)
                     nc.sync.dma_start(out=bias_rows[0:M_TILES, :], in_=b.rearrange("(m p) -> m p", p=P))
+        load_w(0, 1)
+        load_w(0, 2)
+        nc.sync.dma_start(lists_out[:], offs2)
         nc.sync.dma_start(out=wgo_sb[:], in_=wgo)
         for m in range(1, M_TILES):
-            load_w(m)
+            for a in range(PASSES):
+                load_w(m, a)
 
         for m in range(M_TILES - 1):
             nc.vector.memset(window[m][:].bitcast(U32), 0)
@@ -157,40 +212,44 @@ def tile_list_hboth_gelu_kernel(tc, xT, w, wgt, b, wgo, offs, offs2, out):
         nc.tensor.transpose(bias_bank[:], bias_rows[:], ident[:])
         nc.scalar.copy(out=bias[:], in_=bias_bank[:, 0:M_TILES])
 
-        for a in range(LAST):
+        for a in range(PASSES):
             for i in range(PACK):
-                for entries in (slice(0, S // 2), slice(S // 2, S)) if (a, i) == (0, 0) else (everything,):
-                    gather(picked[a][:, i, entries], x[a][i], entries)
-            interleave(nc.scalar.copy, x_bf[:, a, :, :], picked[a][:])
-        for i in range(PACK):
-            gather(picked_first[:, i, :], x[LAST][i], PIECES[0])
-            gather(picked_rest[:, i, :], x[LAST][i], slice(128, S))
-            if i == PACK - 2:
-                quantize(x_codes_early[:], x_scales_early[:], x_bf[:].rearrange("p a j i -> p (a j i)"))
-                prepare_w(0)
+                if (a, i) == (0, 0):
+                    gather(a, i, slice(0, S // 2))
+                    gather(a, i, slice(S // 2, S))
+                elif (a, i) == (LAST, PACK - 1):
+                    quantize_early(0)
+                    round_w(0, 0)
+                    gather(a, i, PIECES[0])
+                    gather(a, i, slice(P, S))
+                else:
+                    gather(a, i, everything)
+            for n in range(3):
+                grouped = x_bf_early[n][:, a, :, :] if a < LAST else x_bf_last[n][:]
+                interleave(nc.scalar.copy, grouped, picked[a][:, :, PIECES[n]])
 
-        def quantize_last(n):
-            quantize(
-                x_codes_last[:, PIECES[n]], x_scales_last[:, PIECES[n]], x_bf_last[n][:].rearrange("p j i -> p (j i)")
-            )
-
-        interleave(nc.scalar.copy, x_bf_last[0][:], picked_first[:])
+        round_w(0, 1, nc.vector.tensor_copy)
+        quantize_w(0, 0)
+        round_w(0, 2, nc.vector.tensor_copy)
+        quantize_w(0, 1)
+        quantize_w(0, 2)
         quantize_last(0)
-        interleave(nc.scalar.copy, x_bf_last[1][:], picked_rest[:, :, 0:128])
-        interleave(nc.vector.tensor_copy, x_bf_last[2][:], picked_rest[:, :, 128:384])
+        quantize_early(1)
         quantize_last(1)
-        project(0, PIECES[0], acc_first[0], y_first[0])
-        scatter(0, PIECES[0], y_first[0])
+        quantize_early(2)
         quantize_last(2)
-        project(0, PIECES[1], acc_first[1], y_first[1])
-        scatter(0, PIECES[1], y_first[1])
-        prepare_w(1)
-        project(0, PIECES[2], acc_first[2], y_first[2])
-        scatter(0, PIECES[2], y_first[2])
-        store(0)
-        for m in range(1, M_TILES):
-            if m + 1 < M_TILES:
-                prepare_w(m + 1)
-            project(m, everything, acc[m], y[m])
-            scatter(m, everything, y[m])
-            store(m)
+        round_w(1, 0, nc.vector.tensor_copy)
+        quantize_w(1, 0)
+        finish(0, 0)
+        round_w(1, 1)
+        quantize_w(1, 1)
+        finish(0, 1)
+        round_w(1, 2)
+        quantize_w(1, 2)
+        finish(0, 2)
+        prepare_joint(2)
+        finish(1, 0)
+        prepare_joint(3)
+        finish(1, 1)
+        finish(2, 0)
+        finish(3, 0)

@@ -16,13 +16,18 @@ MULT = mybir.AluOpType.mult
 GELU = mybir.ActivationFunctionType.Gelu_apprx_tanh
 
 P = 128
+GROUPS = 8
+GROUP_ROWS = P // GROUPS
 PACK = 4
 K_PASS = P * PACK
 PASSES = K // K_PASS
 LAST = PASSES - 1
 M_TILES = M // P
+BLOCKS = S // P
 COPY_RUN = 4
 ALIGN = 64
+HALF = S // 2
+HALVES = (slice(0, HALF), slice(HALF, S))
 PIECES = (slice(0, 128), slice(128, 256), slice(256, 512))
 WIDTHS = tuple(c.stop - c.start for c in PIECES)
 
@@ -38,32 +43,31 @@ def tile_list_hboth_gelu_kernel(tc, xT, w, wgt, b, wgo, offs, offs2, out):
 
         lists_in = keep.tile([P, S // 16], U16, name="lists_in")
         lists_out = keep.tile([P, S // 16], U16, name="lists_out")
-        bias_rows = sbuf([P, P], F32, "bias_rows")
+        rows = sbuf([P, S], F32, "rows")
         ident = sbuf([P, P], F32, "ident")
         bias = sbuf([P, M_TILES], F32, "bias")
         scratch = sbuf([P, 2], F32, "scratch")
         wgt_sb = sbuf([P, S], F32, "wgt_sb")
+        wgo_turned = sbuf([P, BLOCKS, GROUPS, GROUP_ROWS], F32, "wgo_turned")
         wgo_sb = sbuf([P, S], F32, "wgo_sb")
         x = [[sbuf([P, T], F32, f"x{a}_{i}") for i in range(PACK)] for a in range(PASSES)]
-        w_raw_joint = [sbuf([P, PASSES, PACK, P], F32, f"w_raw{m}") if m >= 2 else None for m in range(M_TILES)]
-        w_raw = [
-            [
-                w_raw_joint[m][:, a, :, :] if m >= 2 else sbuf([P, PACK, P], F32, f"w_raw{m}_{a}")[:]
-                for a in range(PASSES)
-            ]
-            for m in range(M_TILES)
-        ]
+        w_raw = [[sbuf([P, PACK, P], F32, f"w_raw{m}_{a}") for a in range(PASSES)] for m in range(M_TILES)]
         window = [keep.tile([P, T], F32, name=f"window{m}") for m in range(M_TILES)]
         picked = [sbuf([P, PACK, S], F32, f"picked{a}") for a in range(PASSES)]
         x_bf_early = [sbuf([P, LAST, WIDTHS[n], PACK], BF16, f"x_bf_early{n}") for n in range(3)]
         x_bf_last = [sbuf([P, WIDTHS[n], PACK], BF16, f"x_bf_last{n}") for n in range(3)]
-        w_bf = [[sbuf([P, P, PACK], BF16, f"w_bf{m}_{a}") for a in range(PASSES)] for m in range(2)]
-        w_bf_joint = [sbuf([P, PASSES, P, PACK], BF16, f"w_bf{m}") if m >= 2 else None for m in range(M_TILES)]
-        codes_head = sbuf([P, LAST * P], U32, "codes_head", tag=f"x{LAST}_2")
-        codes_urgent = sbuf([P, 3 * P], U32, "codes_urgent", tag=f"w_raw0_{LAST}")
-        codes_rest = sbuf([P, PASSES * (S - P)], U32, "codes_rest", tag=f"w_bf0_{LAST}")
+        w_bf = [[sbuf([P, P, PACK], BF16, f"w_bf{m}_{a}") for a in range(PASSES)] for m in range(M_TILES)]
+        codes_head = sbuf([P, LAST * P], U32, "codes_head", tag="w_raw0_0")
+        codes_urgent = sbuf([P, 2 * P], U32, "codes_urgent", tag="w_raw0_2")
+        first_codes = codes_urgent[:, P : 2 * P]
+        w0_codes = [
+            sbuf([P, P], U32, "w_codes0_0")[:],
+            sbuf([P, P], U32, "w_codes0_1", tag="x2_3")[:],
+            codes_urgent[:, 0:P],
+        ]
+        codes_rest = sbuf([P, PASSES * (S - P)], U32, "codes_rest", tag="w_bf0_2")
         early_codes = [codes_head[:], codes_rest[:, 0:256], codes_rest[:, 256:768]]
-        last_codes = [codes_urgent[:, 2 * P : 3 * P], codes_rest[:, 768:896], codes_rest[:, 896:1152]]
+        last_codes = [first_codes, codes_rest[:, 768:896], codes_rest[:, 896:1152]]
         early_scales = [sbuf([P, LAST * WIDTHS[n]], U8, f"early_scales{n}") for n in range(3)]
         last_scales = [sbuf([P, WIDTHS[n]], U8, f"last_scales{n}") for n in range(3)]
         x_codes = [
@@ -72,36 +76,18 @@ def tile_list_hboth_gelu_kernel(tc, xT, w, wgt, b, wgo, offs, offs2, out):
         x_scales = [
             [early_scales[n][:, a * WIDTHS[n] : (a + 1) * WIDTHS[n]] for n in range(3)] for a in range(LAST)
         ] + [[last_scales[n][:] for n in range(3)]]
-        w_codes = [
-            [
-                codes_urgent[:, (a - 1) * P : a * P]
-                if m == 0 and a > 0
-                else sbuf([P, P], U32, f"w_codes{m}_{a}", tag="x2_3" if m == 0 else None)[:]
-                for a in range(PASSES)
-            ]
-            for m in range(2)
+        w_codes = [w0_codes] + [
+            [sbuf([P, P], U32, f"w_codes{m}_{a}")[:] for a in range(PASSES)] for m in range(1, M_TILES)
         ]
-        w_scales = [[sbuf([P, P], U8, f"w_scales{m}_{a}")[:] for a in range(PASSES)] for m in range(2)]
-        codes_joint = [sbuf([P, PASSES * P], U32, f"w_codes{m}") if m >= 2 else None for m in range(M_TILES)]
-        scales_joint = [sbuf([P, PASSES * P], U8, f"w_scales{m}") if m >= 2 else None for m in range(M_TILES)]
-        for m in range(2, M_TILES):
-            w_codes.append([codes_joint[m][:, a * P : (a + 1) * P] for a in range(PASSES)])
-            w_scales.append([scales_joint[m][:, a * P : (a + 1) * P] for a in range(PASSES)])
+        w_scales = [[sbuf([P, P], U8, f"w_scales{m}_{a}") for a in range(PASSES)] for m in range(M_TILES)]
         groups = (((0,), (1,), (2,)), ((0, 1), (2,)), ((0, 1, 2),), ((0, 1, 2),))
-        slots = ((None, "w_raw1_1", "w_raw1_2"), ("w_raw2", "w_raw3"), (None,), (None,))
+        slots = ((None, None, "w_raw1_2"), ("w_raw2_2", "w_raw3_1"), ("w_raw3_2",), (None,))
         y = [
-            [
-                None if (m, u) in ((1, 1), (2, 0)) else sbuf([P, sum(WIDTHS[n] for n in g)], F32, f"y{m}_{u}", tag=slots[m][u])[:]
-                for u, g in enumerate(groups[m])
-            ]
+            [sbuf([P, sum(WIDTHS[n] for n in g)], F32, f"y{m}_{u}", tag=slots[m][u]) for u, g in enumerate(groups[m])]
             for m in range(M_TILES)
         ]
-        y_late = sbuf([P, S // 2 + S], F32, "y_late", tag="w_raw3")
-        y[1].pop()
-        y[1].append(y_late[:, 0 : S // 2])
-        y[2].pop()
-        y[2].append(y_late[:, S // 2 : S // 2 + S])
-        bias_bank = psum.tile([P, P], F32, name="bias_bank", tag="acc3_0")
+        turn_bank = psum.tile([P, BLOCKS, P], F32, name="turn_bank", tag="acc2_0")
+        back_bank = psum.tile([P, BLOCKS, P], F32, name="back_bank", tag="acc3_0")
         acc = [
             [
                 psum.tile([P, sum(WIDTHS[n] for n in g)], F32, name=f"acc{m}_{u}", tag=f"acc{m}_{u}")
@@ -118,8 +104,8 @@ def tile_list_hboth_gelu_kernel(tc, xT, w, wgt, b, wgo, offs, offs2, out):
             nc.sync.dma_start(out=x[a][i][:], in_=planes[:, i, :])
 
         def load_w(m, a):
-            rows = w[a * K_PASS : (a + 1) * K_PASS, m * P : (m + 1) * P]
-            nc.sync.dma_start(out=w_raw[m][a], in_=rows.rearrange("(p i) n -> p i n", i=PACK))
+            part = w[a * K_PASS : (a + 1) * K_PASS, m * P : (m + 1) * P]
+            nc.sync.dma_start(out=w_raw[m][a][:], in_=part.rearrange("(p i) n -> p i n", i=PACK))
 
         def gather(a, i, entries):
             nc.vector.tensor_tensor(
@@ -136,22 +122,14 @@ def tile_list_hboth_gelu_kernel(tc, xT, w, wgt, b, wgo, offs, offs2, out):
             nc.vector.quantize_mx(out=codes.bitcast(FP8X4), scales=scales, in_=grouped)
 
         def round_w(m, a, copy=nc.scalar.copy):
-            interleave(copy, w_bf[m][a][:], w_raw[m][a])
+            interleave(copy, w_bf[m][a][:], w_raw[m][a][:])
 
         def quantize_w(m, a):
-            quantize(w_codes[m][a], w_scales[m][a], w_bf[m][a][:].rearrange("p n i -> p (n i)"))
+            quantize(w_codes[m][a], w_scales[m][a][:], w_bf[m][a][:].rearrange("p n i -> p (n i)"))
 
-        def prepare_joint(m):
-            nc.scalar.copy(
-                out=w_bf_joint[m][:].rearrange("p a (c r) i -> p a c i r", r=COPY_RUN),
-                in_=w_raw_joint[m][:].rearrange("p a i (c r) -> p a c i r", r=COPY_RUN),
-            )
-            for lo, hi in ((0, LAST), (LAST, PASSES)):
-                quantize(
-                    codes_joint[m][:, lo * P : hi * P],
-                    scales_joint[m][:, lo * P : hi * P],
-                    w_bf_joint[m][:, lo:hi, :, :].rearrange("p a n i -> p (a n i)"),
-                )
+        def prepare_w(m, a):
+            round_w(m, a)
+            quantize_w(m, a)
 
         def quantize_early(n):
             quantize(early_codes[n], early_scales[n][:], x_bf_early[n][:].rearrange("p a j i -> p (a j i)"))
@@ -166,16 +144,16 @@ def tile_list_hboth_gelu_kernel(tc, xT, w, wgt, b, wgo, offs, offs2, out):
                     nc.tensor.matmul_mx(
                         out=acc[m][u][:, PIECES[n].start - first : PIECES[n].stop - first],
                         lhsT=w_codes[m][a].bitcast(FP8X4),
-                        lhsT_scale=w_scales[m][a],
+                        lhsT_scale=w_scales[m][a][:],
                         rhs=x_codes[a][n].bitcast(FP8X4),
                         rhs_scale=x_scales[a][n],
                         start=(a == 0 and n == groups[m][u][0]),
                         stop=(a == LAST and n == groups[m][u][-1]),
                     )
-            nc.scalar.activation(y[m][u], acc[m][u][:], GELU, bias=bias[:, m : m + 1])
+            nc.scalar.activation(y[m][u][:], acc[m][u][:], GELU, bias=bias[:, m : m + 1])
             entries = slice(first, PIECES[groups[m][u][-1]].stop)
             nc.vector.tensor_tensor(
-                window[m][:].indirect(lists_out[:, list_cols(entries)]), y[m][u], wgo_sb[:, entries], MULT
+                window[m][:].indirect(lists_out[:, list_cols(entries)]), y[m][u][:], wgo_sb[:, entries], MULT
             )
             if u == len(groups[m]) - 1:
                 nc.sync.dma_start(out=out[m * P : (m + 1) * P, :], in_=window[m][:])
@@ -183,73 +161,89 @@ def tile_list_hboth_gelu_kernel(tc, xT, w, wgt, b, wgo, offs, offs2, out):
         everything = slice(0, S)
 
         nc.gpsimd.memset(scratch[:], 0.0)
-        nc.gpsimd.memset(bias_rows[:], 0.0)
+        nc.gpsimd.memset(rows[:], 0.0)
         nc.scalar.activation(scratch[:, 1:2], scratch[:, 0:1], GELU)
 
         nc.sync.dma_start(lists_in[:], offs)
-        nc.scalar.dma_start(out=wgt_sb[:, 0 : S // 2], in_=wgt[:, 0 : S // 2])
+        nc.scalar.dma_start(out=wgt_sb[:, HALVES[0]], in_=wgt[:, HALVES[0]])
         for a in range(PASSES):
             for i in range(PACK):
                 if (a, i) == (LAST, PACK - 1):
-                    load_w(0, 0)
+                    for c in range(LAST):
+                        load_w(0, c)
                 load_x(a, i)
                 if (a, i) == (0, 0):
-                    nc.sync.dma_start(out=wgt_sb[:, S // 2 : S], in_=wgt[:, S // 2 : S])
-                    nc.sync.dma_start(out=bias_rows[0:M_TILES, :], in_=b.rearrange("(m p) -> m p", p=P))
-        load_w(0, 1)
+                    nc.sync.dma_start(out=wgt_sb[:, HALVES[1]], in_=wgt[:, HALVES[1]])
+                if (a, i) == (0, 1):
+                    nc.scalar.dma_start(
+                        out=rows[0:GROUPS, :], in_=wgo.rearrange("(g r) j -> g r j", r=GROUP_ROWS)[:, 0, :]
+                    )
+                    nc.scalar.dma_start(
+                        out=rows[GROUPS : GROUPS + M_TILES, 0:P], in_=b.rearrange("(m p) -> m p", p=P)
+                    )
         load_w(0, 2)
+        load_w(1, 0)
         nc.sync.dma_start(lists_out[:], offs2)
-        nc.sync.dma_start(out=wgo_sb[:], in_=wgo)
         for m in range(1, M_TILES):
             for a in range(PASSES):
-                load_w(m, a)
+                if (m, a) != (1, 0):
+                    load_w(m, a)
 
         for m in range(M_TILES - 1):
             nc.vector.memset(window[m][:].bitcast(U32), 0)
         make_identity(nc, ident[:])
         nc.gpsimd.memset(window[M_TILES - 1][:], 0.0)
 
-        nc.tensor.transpose(bias_bank[:], bias_rows[:], ident[:])
-        nc.scalar.copy(out=bias[:], in_=bias_bank[:, 0:M_TILES])
+        for c in range(BLOCKS):
+            nc.tensor.transpose(turn_bank[:, c, :], rows[:, c * P : (c + 1) * P], ident[:])
+        nc.scalar.copy(out=bias[:], in_=turn_bank[:, 0, GROUPS : GROUPS + M_TILES])
+        nc.scalar.copy(
+            out=wgo_turned[:],
+            in_=turn_bank[:, :, 0:GROUPS].unsqueeze(3).to_broadcast([P, BLOCKS, GROUPS, GROUP_ROWS]),
+        )
+        for c in range(BLOCKS):
+            nc.tensor.transpose(back_bank[:, c, :], wgo_turned[:, c, :, :].rearrange("j g r -> j (g r)"), ident[:])
+        nc.scalar.copy(out=wgo_sb[:], in_=back_bank[:].rearrange("p c j -> p (c j)"))
 
         for a in range(PASSES):
             for i in range(PACK):
                 if (a, i) == (0, 0):
-                    gather(a, i, slice(0, S // 2))
-                    gather(a, i, slice(S // 2, S))
+                    gather(a, i, HALVES[0])
+                    gather(a, i, HALVES[1])
                 elif (a, i) == (LAST, PACK - 1):
+                    for c in range(LAST):
+                        round_w(0, c)
+                    quantize_w(0, 0)
                     quantize_early(0)
-                    round_w(0, 0)
-                    gather(a, i, PIECES[0])
-                    gather(a, i, slice(P, S))
+                    for piece in PIECES:
+                        gather(a, i, piece)
                 else:
                     gather(a, i, everything)
             for n in range(3):
                 grouped = x_bf_early[n][:, a, :, :] if a < LAST else x_bf_last[n][:]
                 interleave(nc.scalar.copy, grouped, picked[a][:, :, PIECES[n]])
 
-        round_w(0, 1, nc.vector.tensor_copy)
-        quantize_w(0, 0)
         round_w(0, 2, nc.vector.tensor_copy)
         quantize_w(0, 1)
-        quantize_w(0, 2)
         quantize_last(0)
+        quantize_w(0, 2)
         quantize_early(1)
         quantize_last(1)
         quantize_early(2)
         quantize_last(2)
-        round_w(1, 0, nc.vector.tensor_copy)
-        quantize_w(1, 0)
+        prepare_w(1, 0)
         finish(0, 0)
-        round_w(1, 1)
-        quantize_w(1, 1)
+        prepare_w(1, 1)
         finish(0, 1)
-        round_w(1, 2)
-        quantize_w(1, 2)
+        prepare_w(1, 2)
         finish(0, 2)
-        prepare_joint(2)
+        prepare_w(2, 0)
+        prepare_w(2, 1)
+        prepare_w(2, 2)
         finish(1, 0)
-        prepare_joint(3)
+        prepare_w(3, 0)
+        prepare_w(3, 1)
         finish(1, 1)
+        prepare_w(3, 2)
         finish(2, 0)
         finish(3, 0)

@@ -16,8 +16,8 @@ MULT = mybir.AluOpType.mult
 GELU = mybir.ActivationFunctionType.Gelu_apprx_tanh
 
 P = 128
-GROUPS = 8
-GROUP_ROWS = P // GROUPS
+LISTS = 8
+LIST_ROWS = P // LISTS
 PACK = 4
 K_PASS = P * PACK
 PASSES = K // K_PASS
@@ -26,10 +26,11 @@ M_TILES = M // P
 BLOCKS = S // P
 COPY_RUN = 4
 ALIGN = 64
-HALF = S // 2
-HALVES = (slice(0, HALF), slice(HALF, S))
+HALVES = (slice(0, S // 2), slice(S // 2, S))
 PIECES = (slice(0, 128), slice(128, 256), slice(256, 512))
-WIDTHS = tuple(c.stop - c.start for c in PIECES)
+WIDTHS = tuple(piece.stop - piece.start for piece in PIECES)
+SCATTERS = (((0,), (1,), (2,)), ((0, 1), (2,)), ((0, 1, 2),), ((0, 1, 2),))
+Y_TAGS = ((None, None, "w_raw1_2"), ("w_raw2_2", "w_raw3_1"), ("w_raw3_2",), (None,))
 
 
 def tile_list_hboth_gelu_kernel(tc, xT, w, wgt, b, wgo, offs, offs2, out):
@@ -41,63 +42,67 @@ def tile_list_hboth_gelu_kernel(tc, xT, w, wgt, b, wgo, offs, offs2, out):
         def sbuf(shape, dtype, name, tag=None):
             return keep.tile(shape, dtype, name=name, tag=tag or name, align_bytes=ALIGN)
 
-        lists_in = keep.tile([P, S // 16], U16, name="lists_in")
-        lists_out = keep.tile([P, S // 16], U16, name="lists_out")
+        lists_in = keep.tile([P, S // LIST_ROWS], U16, name="lists_in")
+        lists_out = keep.tile([P, S // LIST_ROWS], U16, name="lists_out")
         rows = sbuf([P, S], F32, "rows")
         ident = sbuf([P, P], F32, "ident")
         bias = sbuf([P, M_TILES], F32, "bias")
-        scratch = sbuf([P, 2], F32, "scratch")
+        zero = sbuf([P, 1], F32, "zero")
         wgt_sb = sbuf([P, S], F32, "wgt_sb")
-        wgo_turned = sbuf([P, BLOCKS, GROUPS, GROUP_ROWS], F32, "wgo_turned")
+        wgo_turned = sbuf([P, BLOCKS, LISTS, LIST_ROWS], F32, "wgo_turned")
         wgo_sb = sbuf([P, S], F32, "wgo_sb")
         x = [[sbuf([P, T], F32, f"x{a}_{i}") for i in range(PACK)] for a in range(PASSES)]
         w_raw = [[sbuf([P, PACK, P], F32, f"w_raw{m}_{a}") for a in range(PASSES)] for m in range(M_TILES)]
         window = [keep.tile([P, T], F32, name=f"window{m}") for m in range(M_TILES)]
         picked = [sbuf([P, PACK, S], F32, f"picked{a}") for a in range(PASSES)]
-        x_bf_early = [sbuf([P, LAST, WIDTHS[n], PACK], BF16, f"x_bf_early{n}") for n in range(3)]
-        x_bf_last = [sbuf([P, WIDTHS[n], PACK], BF16, f"x_bf_last{n}") for n in range(3)]
+        x_bf_early = [sbuf([P, LAST, width, PACK], BF16, f"x_bf_early{n}") for n, width in enumerate(WIDTHS)]
+        x_bf_last = [sbuf([P, width, PACK], BF16, f"x_bf_last{n}") for n, width in enumerate(WIDTHS)]
         w_bf = [[sbuf([P, P, PACK], BF16, f"w_bf{m}_{a}") for a in range(PASSES)] for m in range(M_TILES)]
-        codes_head = sbuf([P, LAST * P], U32, "codes_head", tag="w_raw0_0")
-        codes_urgent = sbuf([P, 2 * P], U32, "codes_urgent", tag="w_raw0_2")
-        first_codes = codes_urgent[:, P : 2 * P]
+
+        codes_head = sbuf([P, LAST * WIDTHS[0]], U32, "codes_head", tag="w_raw0_0")
+        behind_widths = (P, WIDTHS[0], LAST * WIDTHS[1], LAST * WIDTHS[2], WIDTHS[1], WIDTHS[2])
+        codes_behind = sbuf([P, sum(behind_widths)], U32, "codes_behind", tag=f"w_raw0_{LAST}")
+        behind = [
+            codes_behind[:, sum(behind_widths[:n]) : sum(behind_widths[: n + 1])] for n in range(len(behind_widths))
+        ]
         w0_codes = [
             sbuf([P, P], U32, "w_codes0_0")[:],
-            sbuf([P, P], U32, "w_codes0_1", tag="x2_3")[:],
-            codes_urgent[:, 0:P],
+            sbuf([P, P], U32, "w_codes0_1", tag=f"x{LAST}_{PACK - 1}")[:],
+            behind[0],
         ]
-        codes_rest = sbuf([P, PASSES * (S - P)], U32, "codes_rest", tag="w_bf0_2")
-        early_codes = [codes_head[:], codes_rest[:, 0:256], codes_rest[:, 256:768]]
-        last_codes = [first_codes, codes_rest[:, 768:896], codes_rest[:, 896:1152]]
-        early_scales = [sbuf([P, LAST * WIDTHS[n]], U8, f"early_scales{n}") for n in range(3)]
-        last_scales = [sbuf([P, WIDTHS[n]], U8, f"last_scales{n}") for n in range(3)]
+        early_codes = [codes_head[:], behind[2], behind[3]]
+        last_codes = [behind[1], behind[4], behind[5]]
+        early_scales = [sbuf([P, LAST * width], U8, f"early_scales{n}") for n, width in enumerate(WIDTHS)]
+        last_scales = [sbuf([P, width], U8, f"last_scales{n}") for n, width in enumerate(WIDTHS)]
         x_codes = [
-            [early_codes[n][:, a * WIDTHS[n] : (a + 1) * WIDTHS[n]] for n in range(3)] for a in range(LAST)
+            [early_codes[n][:, a * width : (a + 1) * width] for n, width in enumerate(WIDTHS)] for a in range(LAST)
         ] + [last_codes]
         x_scales = [
-            [early_scales[n][:, a * WIDTHS[n] : (a + 1) * WIDTHS[n]] for n in range(3)] for a in range(LAST)
-        ] + [[last_scales[n][:] for n in range(3)]]
+            [early_scales[n][:, a * width : (a + 1) * width] for n, width in enumerate(WIDTHS)] for a in range(LAST)
+        ] + [[scales[:] for scales in last_scales]]
         w_codes = [w0_codes] + [
             [sbuf([P, P], U32, f"w_codes{m}_{a}")[:] for a in range(PASSES)] for m in range(1, M_TILES)
         ]
         w_scales = [[sbuf([P, P], U8, f"w_scales{m}_{a}") for a in range(PASSES)] for m in range(M_TILES)]
-        groups = (((0,), (1,), (2,)), ((0, 1), (2,)), ((0, 1, 2),), ((0, 1, 2),))
-        slots = ((None, None, "w_raw1_2"), ("w_raw2_2", "w_raw3_1"), ("w_raw3_2",), (None,))
         y = [
-            [sbuf([P, sum(WIDTHS[n] for n in g)], F32, f"y{m}_{u}", tag=slots[m][u]) for u, g in enumerate(groups[m])]
+            [
+                sbuf([P, sum(WIDTHS[n] for n in pieces)], F32, f"y{m}_{u}", tag=Y_TAGS[m][u])
+                for u, pieces in enumerate(SCATTERS[m])
+            ]
             for m in range(M_TILES)
         ]
         turn_bank = psum.tile([P, BLOCKS, P], F32, name="turn_bank", tag="acc2_0")
         back_bank = psum.tile([P, BLOCKS, P], F32, name="back_bank", tag="acc3_0")
         acc = [
             [
-                psum.tile([P, sum(WIDTHS[n] for n in g)], F32, name=f"acc{m}_{u}", tag=f"acc{m}_{u}")
-                for u, g in enumerate(groups[m])
+                psum.tile([P, sum(WIDTHS[n] for n in pieces)], F32, name=f"acc{m}_{u}", tag=f"acc{m}_{u}")
+                for u, pieces in enumerate(SCATTERS[m])
             ]
             for m in range(M_TILES)
         ]
 
         def list_cols(entries):
-            return slice(entries.start // 16, entries.stop // 16)
+            return slice(entries.start // LIST_ROWS, entries.stop // LIST_ROWS)
 
         def load_x(a, i):
             planes = xT[a * K_PASS : (a + 1) * K_PASS, :].rearrange("(p i) t -> p i t", i=PACK)
@@ -127,9 +132,10 @@ def tile_list_hboth_gelu_kernel(tc, xT, w, wgt, b, wgo, offs, offs2, out):
         def quantize_w(m, a):
             quantize(w_codes[m][a], w_scales[m][a][:], w_bf[m][a][:].rearrange("p n i -> p (n i)"))
 
-        def prepare_w(m, a):
-            round_w(m, a)
-            quantize_w(m, a)
+        def prepare_w(m, *passes):
+            for a in passes:
+                round_w(m, a)
+                quantize_w(m, a)
 
         def quantize_early(n):
             quantize(early_codes[n], early_scales[n][:], x_bf_early[n][:].rearrange("p a j i -> p (a j i)"))
@@ -138,50 +144,45 @@ def tile_list_hboth_gelu_kernel(tc, xT, w, wgt, b, wgo, offs, offs2, out):
             quantize(last_codes[n], last_scales[n][:], x_bf_last[n][:].rearrange("p j i -> p (j i)"))
 
         def finish(m, u):
-            first = PIECES[groups[m][u][0]].start
+            pieces = SCATTERS[m][u]
+            entries = slice(PIECES[pieces[0]].start, PIECES[pieces[-1]].stop)
             for a in range(PASSES):
-                for n in groups[m][u]:
+                for n in pieces:
                     nc.tensor.matmul_mx(
-                        out=acc[m][u][:, PIECES[n].start - first : PIECES[n].stop - first],
+                        out=acc[m][u][:, PIECES[n].start - entries.start : PIECES[n].stop - entries.start],
                         lhsT=w_codes[m][a].bitcast(FP8X4),
                         lhsT_scale=w_scales[m][a][:],
                         rhs=x_codes[a][n].bitcast(FP8X4),
                         rhs_scale=x_scales[a][n],
-                        start=(a == 0 and n == groups[m][u][0]),
-                        stop=(a == LAST and n == groups[m][u][-1]),
+                        start=(a == 0 and n == pieces[0]),
+                        stop=(a == LAST and n == pieces[-1]),
                     )
             nc.scalar.activation(y[m][u][:], acc[m][u][:], GELU, bias=bias[:, m : m + 1])
-            entries = slice(first, PIECES[groups[m][u][-1]].stop)
             nc.vector.tensor_tensor(
                 window[m][:].indirect(lists_out[:, list_cols(entries)]), y[m][u][:], wgo_sb[:, entries], MULT
             )
-            if u == len(groups[m]) - 1:
+            if u == len(SCATTERS[m]) - 1:
                 nc.sync.dma_start(out=out[m * P : (m + 1) * P, :], in_=window[m][:])
 
-        everything = slice(0, S)
-
-        nc.gpsimd.memset(scratch[:], 0.0)
-        nc.gpsimd.memset(rows[:], 0.0)
-        nc.scalar.activation(scratch[:, 1:2], scratch[:, 0:1], GELU)
+        nc.gpsimd.memset(zero[:], 0.0)
+        nc.scalar.activation(rows[:], zero[:].to_broadcast([P, S]), GELU)
 
         nc.sync.dma_start(lists_in[:], offs)
         nc.scalar.dma_start(out=wgt_sb[:, HALVES[0]], in_=wgt[:, HALVES[0]])
         for a in range(PASSES):
             for i in range(PACK):
                 if (a, i) == (LAST, PACK - 1):
-                    for c in range(LAST):
-                        load_w(0, c)
+                    for early in range(LAST):
+                        load_w(0, early)
                 load_x(a, i)
                 if (a, i) == (0, 0):
                     nc.sync.dma_start(out=wgt_sb[:, HALVES[1]], in_=wgt[:, HALVES[1]])
                 if (a, i) == (0, 1):
                     nc.scalar.dma_start(
-                        out=rows[0:GROUPS, :], in_=wgo.rearrange("(g r) j -> g r j", r=GROUP_ROWS)[:, 0, :]
+                        out=rows[0:LISTS, :], in_=wgo.rearrange("(g r) j -> g r j", r=LIST_ROWS)[:, 0, :]
                     )
-                    nc.scalar.dma_start(
-                        out=rows[GROUPS : GROUPS + M_TILES, 0:P], in_=b.rearrange("(m p) -> m p", p=P)
-                    )
-        load_w(0, 2)
+                    nc.scalar.dma_start(out=rows[LISTS : LISTS + M_TILES, 0:P], in_=b.rearrange("(m p) -> m p", p=P))
+        load_w(0, LAST)
         load_w(1, 0)
         nc.sync.dma_start(lists_out[:], offs2)
         for m in range(1, M_TILES):
@@ -196,10 +197,10 @@ def tile_list_hboth_gelu_kernel(tc, xT, w, wgt, b, wgo, offs, offs2, out):
 
         for c in range(BLOCKS):
             nc.tensor.transpose(turn_bank[:, c, :], rows[:, c * P : (c + 1) * P], ident[:])
-        nc.scalar.copy(out=bias[:], in_=turn_bank[:, 0, GROUPS : GROUPS + M_TILES])
+        nc.scalar.copy(out=bias[:], in_=turn_bank[:, 0, LISTS : LISTS + M_TILES])
         nc.scalar.copy(
             out=wgo_turned[:],
-            in_=turn_bank[:, :, 0:GROUPS].unsqueeze(3).to_broadcast([P, BLOCKS, GROUPS, GROUP_ROWS]),
+            in_=turn_bank[:, :, 0:LISTS].unsqueeze(3).to_broadcast([P, BLOCKS, LISTS, LIST_ROWS]),
         )
         for c in range(BLOCKS):
             nc.tensor.transpose(back_bank[:, c, :], wgo_turned[:, c, :, :].rearrange("j g r -> j (g r)"), ident[:])
@@ -208,41 +209,38 @@ def tile_list_hboth_gelu_kernel(tc, xT, w, wgt, b, wgo, offs, offs2, out):
         for a in range(PASSES):
             for i in range(PACK):
                 if (a, i) == (0, 0):
-                    gather(a, i, HALVES[0])
-                    gather(a, i, HALVES[1])
+                    for entries in HALVES:
+                        gather(a, i, entries)
                 elif (a, i) == (LAST, PACK - 1):
-                    for c in range(LAST):
-                        round_w(0, c)
+                    for early in range(LAST):
+                        round_w(0, early)
                     quantize_w(0, 0)
                     quantize_early(0)
-                    for piece in PIECES:
-                        gather(a, i, piece)
+                    for entries in PIECES:
+                        gather(a, i, entries)
                 else:
-                    gather(a, i, everything)
-            for n in range(3):
+                    gather(a, i, slice(0, S))
+            for n, entries in enumerate(PIECES):
                 grouped = x_bf_early[n][:, a, :, :] if a < LAST else x_bf_last[n][:]
-                interleave(nc.scalar.copy, grouped, picked[a][:, :, PIECES[n]])
+                interleave(nc.scalar.copy, grouped, picked[a][:, :, entries])
 
-        round_w(0, 2, nc.vector.tensor_copy)
+        round_w(0, LAST, nc.vector.tensor_copy)
         quantize_w(0, 1)
         quantize_last(0)
-        quantize_w(0, 2)
-        quantize_early(1)
-        quantize_last(1)
-        quantize_early(2)
-        quantize_last(2)
+        quantize_w(0, LAST)
+        for n in (1, 2):
+            quantize_early(n)
+            quantize_last(n)
+
         prepare_w(1, 0)
         finish(0, 0)
         prepare_w(1, 1)
         finish(0, 1)
         prepare_w(1, 2)
         finish(0, 2)
-        prepare_w(2, 0)
-        prepare_w(2, 1)
-        prepare_w(2, 2)
+        prepare_w(2, 0, 1, 2)
         finish(1, 0)
-        prepare_w(3, 0)
-        prepare_w(3, 1)
+        prepare_w(3, 0, 1)
         finish(1, 1)
         prepare_w(3, 2)
         finish(2, 0)

@@ -190,10 +190,9 @@ def tile_list_hboth_gelu_kernel(tc, xT, w, wgt, b, wgo, offs, offs2, out):
                 if (m, a) != (1, 0):
                     load_w(m, a)
 
-        for m in range(M_TILES - 1):
-            nc.vector.memset(window[m][:].bitcast(U32), 0)
         make_identity(nc, ident[:])
-        nc.gpsimd.memset(window[M_TILES - 1][:], 0.0)
+        for m in range(M_TILES):
+            nc.gpsimd.memset(window[m][:], 0.0)
 
         for c in range(BLOCKS):
             nc.tensor.transpose(turn_bank[:, c, :], rows[:, c * P : (c + 1) * P], ident[:])

@@ -23,14 +23,14 @@ K_PASS = P * PACK
 PASSES = K // K_PASS
 LAST = PASSES - 1
 M_TILES = M // P
-BLOCKS = S // P
+BLOCKS = S // 2 // P
 COPY_RUN = 4
 ALIGN = 64
 HALVES = (slice(0, S // 2), slice(S // 2, S))
 PIECES = (slice(0, 128), slice(128, 256), slice(256, 512))
 WIDTHS = tuple(piece.stop - piece.start for piece in PIECES)
 SCATTERS = (((0,), (1,), (2,)), ((0, 1), (2,)), ((0, 1, 2),), ((0, 1, 2),))
-Y_TAGS = ((None, None, "w_raw1_2"), ("w_raw2_2", "w_raw3_1"), ("w_raw3_2",), (None,))
+Y_TAGS = ((None, None, None), ("w_raw2_2", "w_raw3_1"), ("w_raw3_2",), (None,))
 
 
 def tile_list_hboth_gelu_kernel(tc, xT, w, wgt, b, wgo, offs, offs2, out):
@@ -44,7 +44,7 @@ def tile_list_hboth_gelu_kernel(tc, xT, w, wgt, b, wgo, offs, offs2, out):
 
         lists_in = keep.tile([P, S // LIST_ROWS], U16, name="lists_in")
         lists_out = keep.tile([P, S // LIST_ROWS], U16, name="lists_out")
-        rows = sbuf([P, S], F32, "rows")
+        rows = sbuf([P, S // 2], F32, "rows")
         ident = sbuf([P, P], F32, "ident")
         bias = sbuf([P, M_TILES], F32, "bias")
         zero = sbuf([P, 1], F32, "zero")
@@ -165,7 +165,7 @@ def tile_list_hboth_gelu_kernel(tc, xT, w, wgt, b, wgo, offs, offs2, out):
                 nc.sync.dma_start(out=out[m * P : (m + 1) * P, :], in_=window[m][:])
 
         nc.gpsimd.memset(zero[:], 0.0)
-        nc.scalar.activation(rows[:], zero[:].to_broadcast([P, S]), GELU)
+        nc.scalar.activation(rows[:], zero[:].to_broadcast([P, S // 2]), GELU)
 
         nc.sync.dma_start(lists_in[:], offs)
         nc.scalar.dma_start(out=wgt_sb[:, HALVES[0]], in_=wgt[:, HALVES[0]])
@@ -179,7 +179,7 @@ def tile_list_hboth_gelu_kernel(tc, xT, w, wgt, b, wgo, offs, offs2, out):
                     nc.sync.dma_start(out=wgt_sb[:, HALVES[1]], in_=wgt[:, HALVES[1]])
                 if (a, i) == (0, 1):
                     nc.scalar.dma_start(
-                        out=rows[0:LISTS, :], in_=wgo.rearrange("(g r) j -> g r j", r=LIST_ROWS)[:, 0, :]
+                        out=rows[0:LISTS, :], in_=wgo.rearrange("(g r) j -> g r j", r=LIST_ROWS)[:, 0, HALVES[0]]
                     )
                     nc.scalar.dma_start(out=rows[LISTS : LISTS + M_TILES, 0:P], in_=b.rearrange("(m p) -> m p", p=P))
         load_w(0, LAST)
@@ -189,6 +189,8 @@ def tile_list_hboth_gelu_kernel(tc, xT, w, wgt, b, wgo, offs, offs2, out):
             for a in range(PASSES):
                 if (m, a) != (1, 0):
                     load_w(m, a)
+                if (m, a) == (2, 0):
+                    nc.sync.dma_start(out=wgo_sb[:, HALVES[1]], in_=wgo[:, HALVES[1]])
 
         make_identity(nc, ident[:])
         for m in range(M_TILES):
@@ -203,7 +205,7 @@ def tile_list_hboth_gelu_kernel(tc, xT, w, wgt, b, wgo, offs, offs2, out):
         )
         for c in range(BLOCKS):
             nc.tensor.transpose(back_bank[:, c, :], wgo_turned[:, c, :, :].rearrange("j g r -> j (g r)"), ident[:])
-        nc.scalar.copy(out=wgo_sb[:], in_=back_bank[:].rearrange("p c j -> p (c j)"))
+        nc.scalar.copy(out=wgo_sb[:, HALVES[0]], in_=back_bank[:].rearrange("p c j -> p (c j)"))
 
         for a in range(PASSES):
             for i in range(PACK):
@@ -231,11 +233,10 @@ def tile_list_hboth_gelu_kernel(tc, xT, w, wgt, b, wgo, offs, offs2, out):
             quantize_early(n)
             quantize_last(n)
 
-        prepare_w(1, 0)
         finish(0, 0)
-        prepare_w(1, 1)
+        prepare_w(1, 0)
         finish(0, 1)
-        prepare_w(1, 2)
+        prepare_w(1, 1, 2)
         finish(0, 2)
         prepare_w(2, 0, 1, 2)
         finish(1, 0)

@@ -30,7 +30,7 @@ HALVES = (slice(0, S // 2), slice(S // 2, S))
 PIECES = (slice(0, 128), slice(128, 256), slice(256, 512))
 WIDTHS = tuple(piece.stop - piece.start for piece in PIECES)
 SCATTERS = (((0,), (1,), (2,)), ((0, 1), (2,)), ((0, 1, 2),), ((0, 1, 2),))
-Y_TAGS = ((None, None, None), ("w_raw2_2", "w_raw3_1"), ("w_raw3_2",), (None,))
+Y_TAGS = ((None, None, None), ("w_raw2_2", "w_raw3_2"), (None,), (None,))
 
 
 def tile_list_hboth_gelu_kernel(tc, xT, w, wgt, b, wgo, offs, offs2, out):
@@ -57,7 +57,13 @@ def tile_list_hboth_gelu_kernel(tc, xT, w, wgt, b, wgo, offs, offs2, out):
         picked = [sbuf([P, PACK, S], F32, f"picked{a}") for a in range(PASSES)]
         x_bf_early = [sbuf([P, LAST, width, PACK], BF16, f"x_bf_early{n}") for n, width in enumerate(WIDTHS)]
         x_bf_last = [sbuf([P, width, PACK], BF16, f"x_bf_last{n}") for n, width in enumerate(WIDTHS)]
-        w_bf = [[sbuf([P, P, PACK], BF16, f"w_bf{m}_{a}") for a in range(PASSES)] for m in range(M_TILES)]
+        w_bf = [
+            [
+                sbuf([P, P, PACK], BF16, f"w_bf{m}_{a}", tag="w_raw1_0" if (m, a) == (1, 1) else None)
+                for a in range(PASSES)
+            ]
+            for m in range(M_TILES)
+        ]
 
         codes_head = sbuf([P, LAST * WIDTHS[0]], U32, "codes_head", tag="w_raw0_0")
         behind_widths = (P, WIDTHS[0], LAST * WIDTHS[1], LAST * WIDTHS[2], WIDTHS[1], WIDTHS[2])
@@ -167,7 +173,6 @@ def tile_list_hboth_gelu_kernel(tc, xT, w, wgt, b, wgo, offs, offs2, out):
         nc.gpsimd.memset(zero[:], 0.0)
         nc.scalar.activation(rows[:], zero[:].to_broadcast([P, S // 2]), GELU)
 
-        nc.sync.dma_start(lists_in[:], offs)
         nc.scalar.dma_start(out=wgt_sb[:, HALVES[0]], in_=wgt[:, HALVES[0]])
         for a in range(PASSES):
             for i in range(PACK):
@@ -176,6 +181,7 @@ def tile_list_hboth_gelu_kernel(tc, xT, w, wgt, b, wgo, offs, offs2, out):
                         load_w(0, early)
                 load_x(a, i)
                 if (a, i) == (0, 0):
+                    nc.sync.dma_start(lists_in[:], offs)
                     nc.sync.dma_start(out=wgt_sb[:, HALVES[1]], in_=wgt[:, HALVES[1]])
                 if (a, i) == (0, 1):
                     nc.scalar.dma_start(
@@ -234,14 +240,17 @@ def tile_list_hboth_gelu_kernel(tc, xT, w, wgt, b, wgo, offs, offs2, out):
             quantize_last(n)
 
         finish(0, 0)
-        prepare_w(1, 0)
+        round_w(1, 0)
+        round_w(1, 1, nc.vector.tensor_copy)
+        quantize_w(1, 0)
         finish(0, 1)
-        prepare_w(1, 1, 2)
+        quantize_w(1, 1)
+        prepare_w(1, 2)
+        prepare_w(2, 0)
         finish(0, 2)
-        prepare_w(2, 0, 1, 2)
+        prepare_w(2, 1, 2)
         finish(1, 0)
-        prepare_w(3, 0, 1)
+        prepare_w(3, 0, 1, 2)
         finish(1, 1)
-        prepare_w(3, 2)
         finish(2, 0)
         finish(3, 0)

@@ -25,6 +25,7 @@ LAST = PASSES - 1
 M_TILES = M // P
 BLOCKS = S // 2 // P
 COPY_RUN = 4
+SQUARE = 32
 ALIGN = 64
 HALVES = (slice(0, S // 2), slice(S // 2, S))
 PIECES = (slice(0, 128), slice(128, 256), slice(256, 512))
@@ -49,6 +50,9 @@ def tile_list_hboth_gelu_kernel(tc, xT, w, wgt, b, wgo, offs, offs2, out):
         bias = sbuf([P, M_TILES], F32, "bias")
         zero = sbuf([P, 1], F32, "zero")
         wgt_sb = sbuf([P, S], F32, "wgt_sb")
+        wgt_rows = sbuf([P, SQUARE], F32, "wgt_rows")
+        wgt_turned = sbuf([P, SQUARE], F32, "wgt_turned")
+        wgt_wide = [sbuf([P, S // 2], F32, f"wgt_wide{h}") for h in range(2)]
         wgo_turned = sbuf([P, BLOCKS, LISTS, LIST_ROWS], F32, "wgo_turned")
         wgo_sb = sbuf([P, S], F32, "wgo_sb")
         x = [[sbuf([P, T], F32, f"x{a}_{i}") for i in range(PACK)] for a in range(PASSES)]
@@ -173,7 +177,7 @@ def tile_list_hboth_gelu_kernel(tc, xT, w, wgt, b, wgo, offs, offs2, out):
         nc.gpsimd.memset(zero[:], 0.0)
         nc.scalar.activation(rows[:], zero[:].to_broadcast([P, S // 2]), GELU)
 
-        nc.scalar.dma_start(out=wgt_sb[:, HALVES[0]], in_=wgt[:, HALVES[0]])
+        nc.sync.dma_start(out=wgt_rows[:], in_=wgt.rearrange("(g r) (c j) -> r g c j", r=LIST_ROWS, j=SQUARE)[0])
         for a in range(PASSES):
             for i in range(PACK):
                 if (a, i) == (LAST, PACK - 1):
@@ -182,7 +186,6 @@ def tile_list_hboth_gelu_kernel(tc, xT, w, wgt, b, wgo, offs, offs2, out):
                 load_x(a, i)
                 if (a, i) == (0, 0):
                     nc.sync.dma_start(lists_in[:], offs)
-                    nc.sync.dma_start(out=wgt_sb[:, HALVES[1]], in_=wgt[:, HALVES[1]])
                 if (a, i) == (0, 1):
                     nc.scalar.dma_start(
                         out=rows[0:LISTS, :], in_=wgo.rearrange("(g r) j -> g r j", r=LIST_ROWS)[:, 0, HALVES[0]]
@@ -213,12 +216,19 @@ def tile_list_hboth_gelu_kernel(tc, xT, w, wgt, b, wgo, offs, offs2, out):
             nc.tensor.transpose(back_bank[:, c, :], wgo_turned[:, c, :, :].rearrange("j g r -> j (g r)"), ident[:])
         nc.scalar.copy(out=wgo_sb[:, HALVES[0]], in_=back_bank[:].rearrange("p c j -> p (c j)"))
 
+        nc.vector.transpose(wgt_turned[:], wgt_rows[:])
+        by_run = wgt_turned[:].rearrange("j (u c) -> j c u", u=2)
+        for h in range(2):
+            nc.vector.tensor_copy(
+                out=wgt_wide[h][:].rearrange("j (c u r) -> j c u r", u=2, r=LIST_ROWS),
+                in_=by_run[:, 8 * h : 8 * h + 8, :].unsqueeze(3).to_broadcast([P, 8, 2, LIST_ROWS]),
+            )
+        for h in range(2):
+            nc.vector.transpose(wgt_sb[:, HALVES[h]], wgt_wide[h][:])
+
         for a in range(PASSES):
             for i in range(PACK):
-                if (a, i) == (0, 0):
-                    for entries in HALVES:
-                        gather(a, i, entries)
-                elif (a, i) == (LAST, PACK - 1):
+                if (a, i) == (LAST, PACK - 1):
                     for early in range(LAST):
                         round_w(0, early)
                     quantize_w(0, 0)

@@ -1,7 +1,6 @@
 from contextlib import ExitStack
 
 import concourse.mybir as mybir
-from concourse.masks import make_identity
 
 K, M, T, S = 1536, 512, 1024, 512
 FLOPS = 2 * K * M * S
@@ -45,19 +44,18 @@ def tile_list_hboth_gelu_kernel(tc, xT, w, wgt, b, wgo, offs, offs2, out):
 
         lists_in = keep.tile([P, S // LIST_ROWS], U16, name="lists_in")
         lists_out = keep.tile([P, S // LIST_ROWS], U16, name="lists_out")
-        rows = sbuf([P, S // 2], F32, "rows")
-        ident = sbuf([P, P], F32, "ident")
-        bias = sbuf([P, M_TILES], F32, "bias")
+        b_rows = sbuf([P, SQUARE], F32, "b_rows")
+        bias = sbuf([P, SQUARE], F32, "bias")
         zero = sbuf([P, 1], F32, "zero")
         wgt_sb = sbuf([P, S], F32, "wgt_sb")
         wgt_rows = sbuf([P, SQUARE], F32, "wgt_rows")
         wgt_turned = sbuf([P, SQUARE], F32, "wgt_turned")
         wgt_wide = [sbuf([P, S // 2], F32, f"wgt_wide{h}") for h in range(2)]
-        wgo_turned = sbuf([P, BLOCKS, LISTS, LIST_ROWS], F32, "wgo_turned")
         wgo_sb = sbuf([P, S], F32, "wgo_sb")
         x = [[sbuf([P, T], F32, f"x{a}_{i}") for i in range(PACK)] for a in range(PASSES)]
         w_raw = [[sbuf([P, PACK, P], F32, f"w_raw{m}_{a}") for a in range(PASSES)] for m in range(M_TILES)]
-        window = [keep.tile([P, T], F32, name=f"window{m}") for m in range(M_TILES)]
+        window_tags = ("wgt_turned", "wgt_wide0", "wgt_wide1", "x0_0")
+        window = [sbuf([P, T], F32, f"window{m}", tag=window_tags[m]) for m in range(M_TILES)]
         picked = [sbuf([P, PACK, S], F32, f"picked{a}") for a in range(PASSES)]
         x_bf_early = [sbuf([P, LAST, width, PACK], BF16, f"x_bf_early{n}") for n, width in enumerate(WIDTHS)]
         x_bf_last = [sbuf([P, width, PACK], BF16, f"x_bf_last{n}") for n, width in enumerate(WIDTHS)]
@@ -101,8 +99,6 @@ def tile_list_hboth_gelu_kernel(tc, xT, w, wgt, b, wgo, offs, offs2, out):
             ]
             for m in range(M_TILES)
         ]
-        turn_bank = psum.tile([P, BLOCKS, P], F32, name="turn_bank", tag="acc2_0")
-        back_bank = psum.tile([P, BLOCKS, P], F32, name="back_bank", tag="acc3_0")
         acc = [
             [
                 psum.tile([P, sum(WIDTHS[n] for n in pieces)], F32, name=f"acc{m}_{u}", tag=f"acc{m}_{u}")
@@ -175,8 +171,9 @@ def tile_list_hboth_gelu_kernel(tc, xT, w, wgt, b, wgo, offs, offs2, out):
                 nc.sync.dma_start(out=out[m * P : (m + 1) * P, :], in_=window[m][:])
 
         nc.gpsimd.memset(zero[:], 0.0)
-        nc.scalar.activation(rows[:], zero[:].to_broadcast([P, S // 2]), GELU)
+        nc.scalar.activation(b_rows[:], zero[:].to_broadcast([P, SQUARE]), GELU)
 
+        b_runs = b.rearrange("(m q j) -> q m j", q=P // SQUARE, j=SQUARE)
         nc.sync.dma_start(out=wgt_rows[:], in_=wgt.rearrange("(g r) (c j) -> r g c j", r=LIST_ROWS, j=SQUARE)[0])
         for a in range(PASSES):
             for i in range(PACK):
@@ -186,35 +183,19 @@ def tile_list_hboth_gelu_kernel(tc, xT, w, wgt, b, wgo, offs, offs2, out):
                 load_x(a, i)
                 if (a, i) == (0, 0):
                     nc.sync.dma_start(lists_in[:], offs)
-                if (a, i) == (0, 1):
-                    nc.scalar.dma_start(
-                        out=rows[0:LISTS, :], in_=wgo.rearrange("(g r) j -> g r j", r=LIST_ROWS)[:, 0, HALVES[0]]
-                    )
-                    nc.scalar.dma_start(out=rows[LISTS : LISTS + M_TILES, 0:P], in_=b.rearrange("(m p) -> m p", p=P))
+                if a == 1:
+                    nc.sync.dma_start(out=b_rows[i * SQUARE : i * SQUARE + M_TILES, :], in_=b_runs[i])
+                if (a, i) == (LAST, 0):
+                    nc.sync.dma_start(lists_out[:], offs2)
         load_w(0, LAST)
         load_w(1, 0)
-        nc.sync.dma_start(lists_out[:], offs2)
+        nc.sync.dma_start(out=wgo_sb[:, HALVES[0]], in_=wgo[:, HALVES[0]])
         for m in range(1, M_TILES):
             for a in range(PASSES):
                 if (m, a) != (1, 0):
                     load_w(m, a)
                 if (m, a) == (2, 0):
                     nc.sync.dma_start(out=wgo_sb[:, HALVES[1]], in_=wgo[:, HALVES[1]])
-
-        make_identity(nc, ident[:])
-        for m in range(M_TILES):
-            nc.gpsimd.memset(window[m][:], 0.0)
-
-        for c in range(BLOCKS):
-            nc.tensor.transpose(turn_bank[:, c, :], rows[:, c * P : (c + 1) * P], ident[:])
-        nc.scalar.copy(out=bias[:], in_=turn_bank[:, 0, LISTS : LISTS + M_TILES])
-        nc.scalar.copy(
-            out=wgo_turned[:],
-            in_=turn_bank[:, :, 0:LISTS].unsqueeze(3).to_broadcast([P, BLOCKS, LISTS, LIST_ROWS]),
-        )
-        for c in range(BLOCKS):
-            nc.tensor.transpose(back_bank[:, c, :], wgo_turned[:, c, :, :].rearrange("j g r -> j (g r)"), ident[:])
-        nc.scalar.copy(out=wgo_sb[:, HALVES[0]], in_=back_bank[:].rearrange("p c j -> p (c j)"))
 
         nc.vector.transpose(wgt_turned[:], wgt_rows[:])
         by_run = wgt_turned[:].rearrange("j (u c) -> j c u", u=2)
@@ -225,6 +206,8 @@ def tile_list_hboth_gelu_kernel(tc, xT, w, wgt, b, wgo, offs, offs2, out):
             )
         for h in range(2):
             nc.vector.transpose(wgt_sb[:, HALVES[h]], wgt_wide[h][:])
+        for m in range(M_TILES - 1):
+            nc.gpsimd.memset(window[m][:], 0.0)
 
         for a in range(PASSES):
             for i in range(PACK):
@@ -237,11 +220,14 @@ def tile_list_hboth_gelu_kernel(tc, xT, w, wgt, b, wgo, offs, offs2, out):
                         gather(a, i, entries)
                 else:
                     gather(a, i, slice(0, S))
+                if (a, i) == (0, 0):
+                    nc.gpsimd.memset(window[M_TILES - 1][:], 0.0)
             for n, entries in enumerate(PIECES):
                 grouped = x_bf_early[n][:, a, :, :] if a < LAST else x_bf_last[n][:]
                 interleave(nc.scalar.copy, grouped, picked[a][:, :, entries])
 
         round_w(0, LAST, nc.vector.tensor_copy)
+        nc.vector.transpose(bias[:], b_rows[:])
         quantize_w(0, 1)
         quantize_last(0)
         quantize_w(0, LAST)

@@ -25,6 +25,8 @@ M_TILES = M // P
 BLOCKS = S // 2 // P
 COPY_RUN = 4
 SQUARE = 32
+B_STEP = SQUARE // M_TILES
+WINDOWS = 3
 ALIGN = 64
 HALVES = (slice(0, S // 2), slice(S // 2, S))
 PIECES = (slice(0, 128), slice(128, 256), slice(256, 512))
@@ -54,8 +56,8 @@ def tile_list_hboth_gelu_kernel(tc, xT, w, wgt, b, wgo, offs, offs2, out):
         wgo_sb = sbuf([P, S], F32, "wgo_sb")
         x = [[sbuf([P, T], F32, f"x{a}_{i}") for i in range(PACK)] for a in range(PASSES)]
         w_raw = [[sbuf([P, PACK, P], F32, f"w_raw{m}_{a}") for a in range(PASSES)] for m in range(M_TILES)]
-        window_tags = ("wgt_turned", "wgt_wide0", "wgt_wide1", "x0_0")
-        window = [sbuf([P, T], F32, f"window{m}", tag=window_tags[m]) for m in range(M_TILES)]
+        windows = [sbuf([P, T], F32, f"window{n}") for n in range(WINDOWS)]
+        window = [windows[m % WINDOWS] for m in range(M_TILES)]
         picked = [sbuf([P, PACK, S], F32, f"picked{a}") for a in range(PASSES)]
         x_bf_early = [sbuf([P, LAST, width, PACK], BF16, f"x_bf_early{n}") for n, width in enumerate(WIDTHS)]
         x_bf_last = [sbuf([P, width, PACK], BF16, f"x_bf_last{n}") for n, width in enumerate(WIDTHS)]
@@ -163,7 +165,7 @@ def tile_list_hboth_gelu_kernel(tc, xT, w, wgt, b, wgo, offs, offs2, out):
                         start=(a == 0 and n == pieces[0]),
                         stop=(a == LAST and n == pieces[-1]),
                     )
-            nc.scalar.activation(y[m][u][:], acc[m][u][:], GELU, bias=bias[:, m : m + 1])
+            nc.scalar.activation(y[m][u][:], acc[m][u][:], GELU, bias=bias[:, m * B_STEP : m * B_STEP + 1])
             nc.vector.tensor_tensor(
                 window[m][:].indirect(lists_out[:, list_cols(entries)]), y[m][u][:], wgo_sb[:, entries], MULT
             )
@@ -171,6 +173,8 @@ def tile_list_hboth_gelu_kernel(tc, xT, w, wgt, b, wgo, offs, offs2, out):
                 nc.sync.dma_start(out=out[m * P : (m + 1) * P, :], in_=window[m][:])
 
         nc.gpsimd.memset(zero[:], 0.0)
+        for cleared in windows:
+            nc.vector.memset(cleared[:].bitcast(mybir.dt.int32), 0)
         nc.scalar.activation(b_rows[:], zero[:].to_broadcast([P, SQUARE]), GELU)
 
         b_runs = b.rearrange("(m q j) -> q m j", q=P // SQUARE, j=SQUARE)
@@ -183,8 +187,8 @@ def tile_list_hboth_gelu_kernel(tc, xT, w, wgt, b, wgo, offs, offs2, out):
                 load_x(a, i)
                 if (a, i) == (0, 0):
                     nc.sync.dma_start(lists_in[:], offs)
-                if a == 1:
-                    nc.sync.dma_start(out=b_rows[i * SQUARE : i * SQUARE + M_TILES, :], in_=b_runs[i])
+                if (a, i) == (1, PACK - 1):
+                    nc.sync.dma_start(out=b_rows[0:P:B_STEP, :], in_=b_runs)
                 if (a, i) == (LAST, 0):
                     nc.sync.dma_start(lists_out[:], offs2)
         load_w(0, LAST)
@@ -206,8 +210,6 @@ def tile_list_hboth_gelu_kernel(tc, xT, w, wgt, b, wgo, offs, offs2, out):
             )
         for h in range(2):
             nc.vector.transpose(wgt_sb[:, HALVES[h]], wgt_wide[h][:])
-        for m in range(M_TILES - 1):
-            nc.gpsimd.memset(window[m][:], 0.0)
 
         for a in range(PASSES):
             for i in range(PACK):
@@ -220,8 +222,6 @@ def tile_list_hboth_gelu_kernel(tc, xT, w, wgt, b, wgo, offs, offs2, out):
                         gather(a, i, entries)
                 else:
                     gather(a, i, slice(0, S))
-                if (a, i) == (0, 0):
-                    nc.gpsimd.memset(window[M_TILES - 1][:], 0.0)
             for n, entries in enumerate(PIECES):
                 grouped = x_bf_early[n][:, a, :, :] if a < LAST else x_bf_last[n][:]
                 interleave(nc.scalar.copy, grouped, picked[a][:, :, entries])

@@ -27,7 +27,7 @@ COPY_RUN = 4
 SQUARE = 32
 B_STEP = SQUARE // M_TILES
 WINDOWS = 3
-ALIGN = 64
+ALIGN = 256
 HALVES = (slice(0, S // 2), slice(S // 2, S))
 PIECES = (slice(0, 128), slice(128, 256), slice(256, 512))
 WIDTHS = tuple(piece.stop - piece.start for piece in PIECES)

@@ -56,7 +56,7 @@ def tile_list_hboth_gelu_kernel(tc, xT, w, wgt, b, wgo, offs, offs2, out):
         wgo_sb = sbuf([P, S], F32, "wgo_sb")
         x = [[sbuf([P, T], F32, f"x{a}_{i}") for i in range(PACK)] for a in range(PASSES)]
         w_raw = [[sbuf([P, PACK, P], F32, f"w_raw{m}_{a}") for a in range(PASSES)] for m in range(M_TILES)]
-        windows = [sbuf([P, T], F32, f"window{n}") for n in range(WINDOWS)]
+        windows = [sbuf([P, T], F32, f"window{n}", tag=tag) for n, tag in enumerate((None, None, "wgt_wide1"))]
         window = [windows[m % WINDOWS] for m in range(M_TILES)]
         picked = [sbuf([P, PACK, S], F32, f"picked{a}") for a in range(PASSES)]
         x_bf_early = [sbuf([P, LAST, width, PACK], BF16, f"x_bf_early{n}") for n, width in enumerate(WIDTHS)]
@@ -173,7 +173,7 @@ def tile_list_hboth_gelu_kernel(tc, xT, w, wgt, b, wgo, offs, offs2, out):
                 nc.sync.dma_start(out=out[m * P : (m + 1) * P, :], in_=window[m][:])
 
         nc.gpsimd.memset(zero[:], 0.0)
-        for cleared in windows:
+        for cleared in windows[:-1]:
             nc.vector.memset(cleared[:].bitcast(mybir.dt.int32), 0)
         nc.scalar.activation(b_rows[:], zero[:].to_broadcast([P, SQUARE]), GELU)
 
@@ -210,6 +210,7 @@ def tile_list_hboth_gelu_kernel(tc, xT, w, wgt, b, wgo, offs, offs2, out):
             )
         for h in range(2):
             nc.vector.transpose(wgt_sb[:, HALVES[h]], wgt_wide[h][:])
+        nc.gpsimd.memset(windows[-1][:].bitcast(mybir.dt.int32), 0)
 
         for a in range(PASSES):
             for i in range(PACK):

from contextlib import ExitStack

import concourse.mybir as mybir

K, M, T, S = 1536, 512, 1024, 512
FLOPS = 2 * K * M * S

F32 = mybir.dt.float32
BF16 = mybir.dt.bfloat16
U32 = mybir.dt.uint32
U16 = mybir.dt.uint16
U8 = mybir.dt.uint8
FP8X4 = mybir.dt.float8_e4m3fn_x4
MULT = mybir.AluOpType.mult
GELU = mybir.ActivationFunctionType.Gelu_apprx_tanh

P = 128
LISTS = 8
LIST_ROWS = P // LISTS
PACK = 4
K_PASS = P * PACK
PASSES = K // K_PASS
LAST = PASSES - 1
M_TILES = M // P
BLOCKS = S // 2 // P
COPY_RUN = 4
SQUARE = 32
B_STEP = SQUARE // M_TILES
WINDOWS = 3
ALIGN = 256
HALVES = (slice(0, S // 2), slice(S // 2, S))
PIECES = (slice(0, 128), slice(128, 256), slice(256, 512))
WIDTHS = tuple(piece.stop - piece.start for piece in PIECES)
SCATTERS = (((0,), (1,), (2,)), ((0, 1), (2,)), ((0, 1, 2),), ((0, 1, 2),))
Y_TAGS = ((None, None, None), ("w_raw2_2", "w_raw3_2"), (None,), (None,))


def tile_list_hboth_gelu_kernel(tc, xT, w, wgt, b, wgo, offs, offs2, out):
    nc = tc.nc
    with ExitStack() as ctx:
        keep = ctx.enter_context(tc.tile_pool(name="keep", bufs=1))
        psum = ctx.enter_context(tc.psum_pool(name="psum", bufs=1))

        def sbuf(shape, dtype, name, tag=None):
            return keep.tile(shape, dtype, name=name, tag=tag or name, align_bytes=ALIGN)

        lists_in = keep.tile([P, S // LIST_ROWS], U16, name="lists_in")
        lists_out = keep.tile([P, S // LIST_ROWS], U16, name="lists_out")
        b_rows = sbuf([P, SQUARE], F32, "b_rows")
        bias = sbuf([P, SQUARE], F32, "bias")
        zero = sbuf([P, 1], F32, "zero")
        wgt_sb = sbuf([P, S], F32, "wgt_sb")
        wgt_rows = sbuf([P, SQUARE], F32, "wgt_rows")
        wgt_turned = sbuf([P, SQUARE], F32, "wgt_turned")
        wgt_wide = [sbuf([P, S // 2], F32, f"wgt_wide{h}") for h in range(2)]
        wgo_sb = sbuf([P, S], F32, "wgo_sb")
        x = [[sbuf([P, T], F32, f"x{a}_{i}") for i in range(PACK)] for a in range(PASSES)]
        w_raw = [[sbuf([P, PACK, P], F32, f"w_raw{m}_{a}") for a in range(PASSES)] for m in range(M_TILES)]
        windows = [sbuf([P, T], F32, f"window{n}", tag=tag) for n, tag in enumerate((None, None, "wgt_wide1"))]
        window = [windows[m % WINDOWS] for m in range(M_TILES)]
        picked = [sbuf([P, PACK, S], F32, f"picked{a}") for a in range(PASSES)]
        x_bf_early = [sbuf([P, LAST, width, PACK], BF16, f"x_bf_early{n}") for n, width in enumerate(WIDTHS)]
        x_bf_last = [sbuf([P, width, PACK], BF16, f"x_bf_last{n}") for n, width in enumerate(WIDTHS)]
        w_bf = [
            [
                sbuf([P, P, PACK], BF16, f"w_bf{m}_{a}", tag="w_raw1_0" if (m, a) == (1, 1) else None)
                for a in range(PASSES)
            ]
            for m in range(M_TILES)
        ]

        codes_head = sbuf([P, LAST * WIDTHS[0]], U32, "codes_head", tag="w_raw0_0")
        behind_widths = (P, WIDTHS[0], LAST * WIDTHS[1], LAST * WIDTHS[2], WIDTHS[1], WIDTHS[2])
        codes_behind = sbuf([P, sum(behind_widths)], U32, "codes_behind", tag=f"w_raw0_{LAST}")
        behind = [
            codes_behind[:, sum(behind_widths[:n]) : sum(behind_widths[: n + 1])] for n in range(len(behind_widths))
        ]
        w0_codes = [
            sbuf([P, P], U32, "w_codes0_0")[:],
            sbuf([P, P], U32, "w_codes0_1", tag=f"x{LAST}_{PACK - 1}")[:],
            behind[0],
        ]
        early_codes = [codes_head[:], behind[2], behind[3]]
        last_codes = [behind[1], behind[4], behind[5]]
        early_scales = [sbuf([P, LAST * width], U8, f"early_scales{n}") for n, width in enumerate(WIDTHS)]
        last_scales = [sbuf([P, width], U8, f"last_scales{n}") for n, width in enumerate(WIDTHS)]
        x_codes = [
            [early_codes[n][:, a * width : (a + 1) * width] for n, width in enumerate(WIDTHS)] for a in range(LAST)
        ] + [last_codes]
        x_scales = [
            [early_scales[n][:, a * width : (a + 1) * width] for n, width in enumerate(WIDTHS)] for a in range(LAST)
        ] + [[scales[:] for scales in last_scales]]
        w_codes = [w0_codes] + [
            [sbuf([P, P], U32, f"w_codes{m}_{a}")[:] for a in range(PASSES)] for m in range(1, M_TILES)
        ]
        w_scales = [[sbuf([P, P], U8, f"w_scales{m}_{a}") for a in range(PASSES)] for m in range(M_TILES)]
        y = [
            [
                sbuf([P, sum(WIDTHS[n] for n in pieces)], F32, f"y{m}_{u}", tag=Y_TAGS[m][u])
                for u, pieces in enumerate(SCATTERS[m])
            ]
            for m in range(M_TILES)
        ]
        acc = [
            [
                psum.tile([P, sum(WIDTHS[n] for n in pieces)], F32, name=f"acc{m}_{u}", tag=f"acc{m}_{u}")
                for u, pieces in enumerate(SCATTERS[m])
            ]
            for m in range(M_TILES)
        ]

        def list_cols(entries):
            return slice(entries.start // LIST_ROWS, entries.stop // LIST_ROWS)

        def load_x(a, i):
            planes = xT[a * K_PASS : (a + 1) * K_PASS, :].rearrange("(p i) t -> p i t", i=PACK)
            nc.sync.dma_start(out=x[a][i][:], in_=planes[:, i, :])

        def load_w(m, a):
            part = w[a * K_PASS : (a + 1) * K_PASS, m * P : (m + 1) * P]
            nc.sync.dma_start(out=w_raw[m][a][:], in_=part.rearrange("(p i) n -> p i n", i=PACK))

        def gather(a, i, entries):
            nc.vector.tensor_tensor(
                picked[a][:, i, entries], x[a][i][:].indirect(lists_in[:, list_cols(entries)]), wgt_sb[:, entries], MULT
            )

        def interleave(copy, grouped, planes):
            copy(
                out=grouped.rearrange("p (c r) i -> p c i r", r=COPY_RUN),
                in_=planes.rearrange("p i (c r) -> p c i r", r=COPY_RUN),
            )

        def quantize(codes, scales, grouped):
            nc.vector.quantize_mx(out=codes.bitcast(FP8X4), scales=scales, in_=grouped)

        def round_w(m, a, copy=nc.scalar.copy):
            interleave(copy, w_bf[m][a][:], w_raw[m][a][:])

        def quantize_w(m, a):
            quantize(w_codes[m][a], w_scales[m][a][:], w_bf[m][a][:].rearrange("p n i -> p (n i)"))

        def prepare_w(m, *passes):
            for a in passes:
                round_w(m, a)
                quantize_w(m, a)

        def quantize_early(n):
            quantize(early_codes[n], early_scales[n][:], x_bf_early[n][:].rearrange("p a j i -> p (a j i)"))

        def quantize_last(n):
            quantize(last_codes[n], last_scales[n][:], x_bf_last[n][:].rearrange("p j i -> p (j i)"))

        def finish(m, u):
            pieces = SCATTERS[m][u]
            entries = slice(PIECES[pieces[0]].start, PIECES[pieces[-1]].stop)
            for a in range(PASSES):
                for n in pieces:
                    nc.tensor.matmul_mx(
                        out=acc[m][u][:, PIECES[n].start - entries.start : PIECES[n].stop - entries.start],
                        lhsT=w_codes[m][a].bitcast(FP8X4),
                        lhsT_scale=w_scales[m][a][:],
                        rhs=x_codes[a][n].bitcast(FP8X4),
                        rhs_scale=x_scales[a][n],
                        start=(a == 0 and n == pieces[0]),
                        stop=(a == LAST and n == pieces[-1]),
                    )
            nc.scalar.activation(y[m][u][:], acc[m][u][:], GELU, bias=bias[:, m * B_STEP : m * B_STEP + 1])
            nc.vector.tensor_tensor(
                window[m][:].indirect(lists_out[:, list_cols(entries)]), y[m][u][:], wgo_sb[:, entries], MULT
            )
            if u == len(SCATTERS[m]) - 1:
                nc.sync.dma_start(out=out[m * P : (m + 1) * P, :], in_=window[m][:])

        nc.gpsimd.memset(zero[:], 0.0)
        for cleared in windows[:-1]:
            nc.vector.memset(cleared[:].bitcast(mybir.dt.int32), 0)
        nc.scalar.activation(b_rows[:], zero[:].to_broadcast([P, SQUARE]), GELU)

        b_runs = b.rearrange("(m q j) -> q m j", q=P // SQUARE, j=SQUARE)
        nc.sync.dma_start(out=wgt_rows[:], in_=wgt.rearrange("(g r) (c j) -> r g c j", r=LIST_ROWS, j=SQUARE)[0])
        for a in range(PASSES):
            for i in range(PACK):
                if (a, i) == (LAST, PACK - 1):
                    for early in range(LAST):
                        load_w(0, early)
                load_x(a, i)
                if (a, i) == (0, 0):
                    nc.sync.dma_start(lists_in[:], offs)
                if (a, i) == (1, PACK - 1):
                    nc.sync.dma_start(out=b_rows[0:P:B_STEP, :], in_=b_runs)
                if (a, i) == (LAST, 0):
                    nc.sync.dma_start(lists_out[:], offs2)
        load_w(0, LAST)
        load_w(1, 0)
        nc.sync.dma_start(out=wgo_sb[:, HALVES[0]], in_=wgo[:, HALVES[0]])
        for m in range(1, M_TILES):
            for a in range(PASSES):
                if (m, a) != (1, 0):
                    load_w(m, a)
                if (m, a) == (2, 0):
                    nc.sync.dma_start(out=wgo_sb[:, HALVES[1]], in_=wgo[:, HALVES[1]])

        nc.vector.transpose(wgt_turned[:], wgt_rows[:])
        by_run = wgt_turned[:].rearrange("j (u c) -> j c u", u=2)
        for h in range(2):
            nc.vector.tensor_copy(
                out=wgt_wide[h][:].rearrange("j (c u r) -> j c u r", u=2, r=LIST_ROWS),
                in_=by_run[:, 8 * h : 8 * h + 8, :].unsqueeze(3).to_broadcast([P, 8, 2, LIST_ROWS]),
            )
        for h in range(2):
            nc.vector.transpose(wgt_sb[:, HALVES[h]], wgt_wide[h][:])
        nc.gpsimd.memset(windows[-1][:].bitcast(mybir.dt.int32), 0)

        for a in range(PASSES):
            for i in range(PACK):
                if (a, i) == (LAST, PACK - 1):
                    for early in range(LAST):
                        round_w(0, early)
                    quantize_w(0, 0)
                    quantize_early(0)
                    for entries in PIECES:
                        gather(a, i, entries)
                else:
                    gather(a, i, slice(0, S))
            for n, entries in enumerate(PIECES):
                grouped = x_bf_early[n][:, a, :, :] if a < LAST else x_bf_last[n][:]
                interleave(nc.scalar.copy, grouped, picked[a][:, :, entries])

        round_w(0, LAST, nc.vector.tensor_copy)
        nc.vector.transpose(bias[:], b_rows[:])
        quantize_w(0, 1)
        quantize_last(0)
        quantize_w(0, LAST)
        for n in (1, 2):
            quantize_early(n)
            quantize_last(n)

        finish(0, 0)
        round_w(1, 0)
        round_w(1, 1, nc.vector.tensor_copy)
        quantize_w(1, 0)
        finish(0, 1)
        quantize_w(1, 1)
        prepare_w(1, 2)
        prepare_w(2, 0)
        finish(0, 2)
        prepare_w(2, 1, 2)
        finish(1, 0)
        prepare_w(3, 0, 1, 2)
        finish(1, 1)
        finish(2, 0)
        finish(3, 0)
